import numpy as np
import ml_dtypes


def mxq(x, axis, fmt="e4m3"):
    dtype, down = {"e4m3": (ml_dtypes.float8_e4m3fn, 7), "e5m2": (ml_dtypes.float8_e5m2, 14)}[fmt]
    v = np.moveaxis(np.asarray(x, np.float32).astype(ml_dtypes.bfloat16).astype(np.float64), axis, -1)
    blocks = v.reshape(v.shape[:-1] + (-1, 32))
    amax = np.abs(blocks).max(-1, keepdims=True)
    byte = np.maximum(np.where(amax > 0, np.frexp(amax)[1] - 1 + 127, 0) - down, 1)
    scale = np.exp2(byte - 127.0)
    codes = (blocks / scale).astype(np.float32).astype(dtype).astype(np.float64)
    return np.moveaxis((codes * scale).reshape(v.shape), -1, axis)


WIDE = False


def mx_kscale(k):
    if not WIDE:
        return np.ones(k)
    levels = np.array([10, -10, 5, -5, 0])
    if k % 512:
        return np.exp2(np.random.permutation(np.resize(levels, k // 32))).repeat(32)
    a = np.empty((k // 512, 16))
    for p in range(k // 512):
        a[p, :8] = np.random.permutation(np.resize(levels, 8))
        for g in range(8):
            far = levels[np.abs(levels - a[p, g]) >= 10]
            a[p, g + 8] = far[np.random.randint(len(far))]
    return np.exp2(a.ravel()).repeat(32)


def f64(x):
    return np.asarray(x).astype(np.float64)


def striped(idx):
    return np.tile(np.asarray(idx).reshape(-1, 16).T, (8, 1)).astype(np.uint16)


def unstriped(offs):
    return offs[:16].T.reshape(-1).astype(np.int64)


B, N, T, D, DV, NQ = 1, 512, 1024, 512, 128, 128
NEW = 256


def setup_inputs():
    n = np.random.standard_normal
    idx = np.random.permutation(T)[:B * N]
    s = mx_kscale(D)[:, None]
    u = np.ones(T)
    u[idx] = mx_kscale(B * N)
    r = np.random.uniform(0.5, 2.0, T)
    k = n((D, T)) / s
    v = n((DV, T)) / (u * r)
    new = np.random.permutation(idx.reshape(B, N)[:, -NEW // B:].reshape(-1))
    return {
        "qT": (n((B, D, NQ)) * s * (0.80 / np.sqrt(D))).astype(np.float32),
        "kT": np.where(np.isin(np.arange(T), new)[None, :], n((D, T)), k).astype(np.float32),
        "vT": np.where(np.isin(np.arange(T), new)[None, :], n((DV, T)), v).astype(np.float32),
        "new_kT": k[:, new].astype(np.float32),
        "new_vT": v[:, new].astype(np.float32),
        "vs": np.tile(u * r, (128, 1)).astype(np.float32),
        "sink": (2.0 + 3.0 * n((B, NQ, 1))).astype(np.float32),
        "offs": striped(idx),
        "slots": striped(new),
    }


def reference(qT, kT, vT, new_kT, new_vT, vs, sink, offs, slots):
    idx = unstriped(offs)
    k = f64(kT)
    k[:, unstriped(slots)] = f64(new_kT)
    v = f64(vT)
    v[:, unstriped(slots)] = f64(new_vT)
    pick = lambda x: x[:, idx].reshape(x.shape[0], B, N).transpose(1, 0, 2)
    q = f64(qT)
    score = mxq(q, 1, "e4m3").transpose(0, 2, 1) @ mxq(pick(k), 1, "e4m3")
    m = np.maximum(score.max(-1, keepdims=True), f64(sink))
    p = np.exp(score - m)
    total = p.sum(-1, keepdims=True) + np.exp(f64(sink) - m)
    w = p * pick(f64(vs))[:, :1, :]
    y = mxq(w, 2, "e4m3") @ mxq(pick(v).transpose(0, 2, 1), 1, "e4m3")
    y = y / total
    return y

@@ -1,0 +1,153 @@
+from contextlib import ExitStack
+
+import concourse.mybir as mybir
+from concourse.masks import make_identity
+
+F32 = mybir.dt.float32
+BF16 = mybir.dt.bfloat16
+U32 = mybir.dt.uint32
+U16 = mybir.dt.uint16
+U8 = mybir.dt.uint8
+FP8X4 = mybir.dt.float8_e4m3fn_x4
+MULT = mybir.AluOpType.mult
+ADD = mybir.AluOpType.add
+MAX = mybir.AluOpType.max
+MIN = mybir.AluOpType.min
+EXP = mybir.ActivationFunctionType.Exp
+COPY = mybir.ActivationFunctionType.Copy
+AXIS_X = mybir.AxisListType.X
+
+P = 128
+N, T, D, DV, NQ, NEW = 512, 1024, 512, 128, 128, 256
+FLOPS = 2 * NQ * N * (D + DV)
+
+
+def tile_attend_kv_append256_sink_kernel(tc, qT, kT, vT, new_kT, new_vT, vs, sink, offs, slots, out):
+    nc = tc.nc
+    with ExitStack() as ctx:
+        held = ctx.enter_context(tc.tile_pool(name="held", bufs=1))
+        psum = ctx.enter_context(tc.psum_pool(name="psum", bufs=1))
+
+        slots_sb = held.tile([P, NEW // 16], U16, name="slots_sb")
+        offs_sb = held.tile([P, N // 16], U16, name="offs_sb")
+        newv = held.tile([P, NEW], F32, name="newv", tag="ring", align_bytes=64)
+        vpool = held.tile([P, T], F32, name="vpool")
+        newk01 = [held.tile([P, NEW], F32, name=f"newk{t}") for t in range(2)]
+        newk23 = held.tile([P, 2, NEW], F32, name="newk23")
+        newk = [newk01[0][:], newk01[1][:], newk23[:, 0, :], newk23[:, 1, :]]
+        kpool = [held.tile([P, T], F32, name=f"kpool{t}", tag=f"kpool{t}", align_bytes=64) for t in range(4)]
+        q_raw = held.tile([P, 4, NQ], F32, name="q_raw")
+        vs_sb = held.tile([P, T], F32, name="vs_sb")
+        sink_sb = held.tile([P, 1], F32, name="sink_sb")
+
+        kT_v = kT.rearrange("(p t) n -> p t n", t=4)
+        newk_v = new_kT.rearrange("(p t) n -> p t n", t=4)
+        for t in range(4):
+            nc.sync.dma_start(kpool[t][:], kT_v[:, t, :])
+            if t < 2:
+                nc.sync.dma_start(newk[t], newk_v[:, t, :])
+            if t == 2:
+                nc.sync.dma_start(newk23[:], newk_v[:, 2:, :])
+            if t == 0:
+                nc.sync.dma_start(slots_sb[:], slots)
+        nc.sync.dma_start(newv[:], new_vT)
+        nc.sync.dma_start(vpool[:], vT)
+        nc.sync.dma_start(q_raw[:], qT.rearrange("b (p t) q -> p (b t) q", t=4))
+        nc.sync.dma_start(offs_sb[:], offs)
+        nc.sync.dma_start(vs_sb[:], vs)
+        nc.scalar.dma_start(sink_sb[:], sink.rearrange("b q o -> (b q) o"))
+
+        ident_f = held.tile([P, P], F32, name="ident_f")
+        make_identity(nc, ident_f[:])
+        warm = held.tile([P, 1], F32, name="warm")
+        nc.gpsimd.memset(warm[:], 0.0)
+        nc.scalar.activation(warm[:], warm[:], EXP)
+
+        kpair = [held.tile([P, 2 * T], BF16, name=f"kpair{u}", tag=f"kpair{u}", align_bytes=64) for u in range(2)]
+        for t in range(4):
+            nc.vector.tensor_copy(kpool[t][:].indirect(slots_sb[:]), newk[t])
+            nc.scalar.copy(kpair[t // 2][:].rearrange("p (n j) -> p n j", j=2)[:, :, t % 2], kpool[t][:])
+
+        nc.vector.tensor_copy(vpool[:].indirect(slots_sb[:]), newv[:])
+        q_b = held.tile([P, NQ, 4], BF16, name="q_b", tag="kpool3", align_bytes=64)
+        nc.scalar.copy(q_b[:], q_raw[:].rearrange("p t q -> p q t"))
+        vpool_b = held.tile([P, T], BF16, name="vpool_b")
+        nc.scalar.copy(vpool_b[:], vpool[:])
+
+        k_g = held.tile([P, N * 4], BF16, name="k_g", tag="ring", align_bytes=64)
+        k_g32 = k_g[:].bitcast(U32).rearrange("p (n u) -> p n u", u=2)
+        for u in range(2):
+            nc.vector.tensor_copy(k_g32[:, :, u], kpair[u][:].bitcast(U32).indirect(offs_sb[:]))
+        q_c = held.tile([P, NQ], U32, name="q_c", tag="kpair1", align_bytes=64)
+        q_s = held.tile([P, NQ], U8, name="q_s", align_bytes=64)
+        nc.vector.quantize_mx(out=q_c[:].bitcast(FP8X4), scales=q_s[:], in_=q_b[:].rearrange("p q t -> p (q t)"))
+        k_c = held.tile([P, N], U32, name="k_c", align_bytes=64)
+        k_s = held.tile([P, N], U8, name="k_s", align_bytes=64)
+        nc.vector.quantize_mx(out=k_c[:].bitcast(FP8X4), scales=k_s[:], in_=k_g[:])
+
+        score = psum.tile([P, N], F32, name="score")
+        nc.tensor.matmul_mx(score[:], lhsT=q_c[:].bitcast(FP8X4), lhsT_scale=q_s[:], rhs=k_c[:].bitcast(FP8X4), rhs_scale=k_s[:], start=True, stop=True)
+
+        v_g = held.tile([P, N], BF16, name="v_g", align_bytes=64)
+        nc.scalar.activation(v_g[:].rearrange("p (u s j) -> p s u j", u=2, j=2), vpool_b[:].indirect(offs_sb[:]), COPY)
+        v_ps = psum.tile([P, 2, DV], F32, name="v_ps")
+        for u in range(2):
+            nc.tensor.transpose(v_ps[:, u, :], v_g[:, u * (N // 2) : (u + 1) * (N // 2)].bitcast(F32), ident_f[:])
+        v_b = held.tile([P, DV * 4], BF16, name="v_b", align_bytes=64)
+        nc.scalar.copy(v_b[:].bitcast(F32).rearrange("p (e u) -> p e u", u=2), v_ps[:].rearrange("p u e -> p e u"))
+
+        negsink = held.tile([P, 1], F32, name="negsink")
+        nc.gpsimd.tensor_scalar(negsink[:], sink_sb[:], -1.0, 0.0, op0=MULT, op1=ADD)
+        vs_g = held.tile([P, N], F32, name="vs_g", tag="ring", align_bytes=64)
+        nc.vector.tensor_copy(vs_g[:], vs_sb[:].indirect(offs_sb[:]))
+        vs_ps = psum.tile([P, 4, P], F32, name="vs_ps")
+        for t in range(4):
+            nc.tensor.transpose(vs_ps[:, t, :], vs_g[:, t::4], ident_f[:])
+
+        negm = held.tile([P, 1], F32, name="negm")
+        neg_score = held.tile([P, N], F32, name="neg_score")
+        nc.vector.tensor_scalar(neg_score[:], score[:], -1.0, negsink[:], op0=MULT, op1=MIN, accum_out=negm[:])
+        vs_col = held.tile([P, 4], F32, name="vs_col")
+        nc.vector.tensor_copy(vs_col[:], vs_ps[:, :, 0])
+
+        p_sb = held.tile([P, 4, P], F32, name="p_sb")
+        l_ab = held.tile([P, 2], F32, name="l_ab")
+        score_v = score[:].rearrange("q (s t) -> q t s", t=4)
+        for h in range(2):
+            nc.scalar.activation(p_sb[:, 2 * h : 2 * h + 2, :], score_v[:, 2 * h : 2 * h + 2, :], EXP, bias=negm[:], accum_out=l_ab[:, h : h + 1])
+
+        v_c = held.tile([P, DV], U32, name="v_c", align_bytes=64)
+        v_s = held.tile([P, DV], U8, name="v_s", align_bytes=64)
+        nc.vector.quantize_mx(out=v_c[:].bitcast(FP8X4), scales=v_s[:], in_=v_b[:])
+
+        w_b = held.tile([P, NQ, 4], BF16, name="w_b", align_bytes=64)
+        w_c = held.tile([P, NQ], U32, name="w_c", align_bytes=64)
+        w_s = held.tile([P, NQ], U8, name="w_s", align_bytes=64)
+        for h in range(2):
+            p_ps = psum.tile([P, 2, NQ], F32, name=f"p_ps{h}")
+            for t in range(2):
+                nc.tensor.transpose(p_ps[:, t, :], p_sb[:, 2 * h + t, :], ident_f[:])
+            for c in ((slice(0, NQ),), (slice(0, NQ // 2), slice(NQ // 2, NQ)))[h]:
+                nc.vector.tensor_tensor(
+                    w_b[:, c, 2 * h : 2 * h + 2],
+                    p_ps[:, :, c].rearrange("s t q -> s q t"),
+                    vs_col[:, 2 * h : 2 * h + 2].unsqueeze(1).to_broadcast([P, c.stop - c.start, 2]),
+                    MULT,
+                )
+        for h in range(2):
+            c = slice(h * NQ // 2, (h + 1) * NQ // 2)
+            nc.vector.quantize_mx(out=w_c[:, c].bitcast(FP8X4), scales=w_s[:, c], in_=w_b[:, c, :].rearrange("p q t -> p (q t)"))
+
+        y_ps = psum.tile([P, DV], F32, name="y_ps")
+        nc.tensor.matmul_mx(y_ps[:], lhsT=w_c[:].bitcast(FP8X4), lhsT_scale=w_s[:], rhs=v_c[:].bitcast(FP8X4), rhs_scale=v_s[:], start=True, stop=True)
+
+        e_sink = held.tile([P, 1], F32, name="e_sink")
+        nc.scalar.activation(e_sink[:], sink_sb[:], EXP, bias=negm[:])
+        l_0 = held.tile([P, 1], F32, name="l_0")
+        nc.vector.scalar_tensor_tensor(l_0[:], l_ab[:, 0:1], e_sink[:], l_ab[:, 1:2], ADD, ADD)
+        r_l = held.tile([P, 1], F32, name="r_l")
+        nc.vector.reciprocal(r_l[:], l_0[:])
+
+        y_sb = held.tile([P, DV], F32, name="y_sb")
+        nc.vector.tensor_scalar(y_sb[:], y_ps[:], r_l[:], None, op0=MULT)
+        nc.sync.dma_start(out.rearrange("b q e -> (b q) e"), y_sb[:])

@@ -42,6 +42,9 @@ def tile_attend_kv_append256_sink_kernel(tc, qT, kT, vT, new_kT, new_vT, vs, sin
 
         kT_v = kT.rearrange("(p t) n -> p t n", t=4)
         newk_v = new_kT.rearrange("(p t) n -> p t n", t=4)
+        nc.sync.dma_start(vs_sb[P - 1 : P, :], vs[0:1, :])
+        nc.vector.memset(vs_sb[: P - 1, :], 0.0)
+        nc.sync.dma_start(offs_sb[:], offs)
         for t in range(4):
             nc.sync.dma_start(kpool[t][:], kT_v[:, t, :])
             if t < 2:
@@ -53,15 +56,21 @@ def tile_attend_kv_append256_sink_kernel(tc, qT, kT, vT, new_kT, new_vT, vs, sin
         nc.sync.dma_start(newv[:], new_vT)
         nc.sync.dma_start(vpool[:], vT)
         nc.sync.dma_start(q_raw[:], qT.rearrange("b (p t) q -> p (b t) q", t=4))
-        nc.sync.dma_start(offs_sb[:], offs)
-        nc.sync.dma_start(vs_sb[:], vs)
-        nc.scalar.dma_start(sink_sb[:], sink.rearrange("b q o -> (b q) o"))
+        nc.sync.dma_start(sink_sb[:], sink.rearrange("b q o -> (b q) o"))
 
         ident_f = held.tile([P, P], F32, name="ident_f")
         make_identity(nc, ident_f[:])
         warm = held.tile([P, 1], F32, name="warm")
         nc.gpsimd.memset(warm[:], 0.0)
         nc.scalar.activation(warm[:], warm[:], EXP)
+
+        vs_g = held.tile([P, N], F32, name="vs_g", align_bytes=64)
+        nc.vector.tensor_copy(vs_g[:], vs_sb[:].indirect(offs_sb[:]))
+        vs_ps = psum.tile([P, 4, P], F32, name="vs_ps")
+        for t in range(4):
+            nc.tensor.transpose(vs_ps[:, t, :], vs_g[:, t::4], ident_f[:])
+        vs_col = held.tile([P, 4], F32, name="vs_col")
+        nc.scalar.copy(vs_col[:], vs_ps[:, :, P - 1])
 
         kpair = [held.tile([P, 2 * T], BF16, name=f"kpair{u}", tag=f"kpair{u}", align_bytes=64) for u in range(2)]
         for t in range(4):
@@ -75,18 +84,19 @@ def tile_attend_kv_append256_sink_kernel(tc, qT, kT, vT, new_kT, new_vT, vs, sin
         nc.scalar.copy(vpool_b[:], vpool[:])
 
         k_g = held.tile([P, N * 4], BF16, name="k_g", tag="ring", align_bytes=64)
-        k_g32 = k_g[:].bitcast(U32).rearrange("p (n u) -> p n u", u=2)
+        k_g32 = k_g[:].bitcast(U32).rearrange("p (h s t u) -> p s h t u", h=2, t=2, u=2)
         for u in range(2):
-            nc.vector.tensor_copy(k_g32[:, :, u], kpair[u][:].bitcast(U32).indirect(offs_sb[:]))
+            nc.vector.tensor_copy(k_g32[:, :, :, :, u], kpair[u][:].bitcast(U32).indirect(offs_sb[:]))
         q_c = held.tile([P, NQ], U32, name="q_c", tag="kpair1", align_bytes=64)
         q_s = held.tile([P, NQ], U8, name="q_s", align_bytes=64)
         nc.vector.quantize_mx(out=q_c[:].bitcast(FP8X4), scales=q_s[:], in_=q_b[:].rearrange("p q t -> p (q t)"))
         k_c = held.tile([P, N], U32, name="k_c", align_bytes=64)
         k_s = held.tile([P, N], U8, name="k_s", align_bytes=64)
-        nc.vector.quantize_mx(out=k_c[:].bitcast(FP8X4), scales=k_s[:], in_=k_g[:])
-
-        score = psum.tile([P, N], F32, name="score")
-        nc.tensor.matmul_mx(score[:], lhsT=q_c[:].bitcast(FP8X4), lhsT_scale=q_s[:], rhs=k_c[:].bitcast(FP8X4), rhs_scale=k_s[:], start=True, stop=True)
+        score = [psum.tile([P, N // 2], F32, name=f"score{h}") for h in range(2)]
+        for h in range(2):
+            c = slice(h * N // 2, (h + 1) * N // 2)
+            nc.vector.quantize_mx(out=k_c[:, c].bitcast(FP8X4), scales=k_s[:, c], in_=k_g[:, 2 * N * h : 2 * N * (h + 1)])
+            nc.tensor.matmul_mx(score[h][:], lhsT=q_c[:].bitcast(FP8X4), lhsT_scale=q_s[:], rhs=k_c[:, c].bitcast(FP8X4), rhs_scale=k_s[:, c], start=True, stop=True)
 
         v_g = held.tile([P, N], BF16, name="v_g", align_bytes=64)
         nc.scalar.activation(v_g[:].rearrange("p (u s j) -> p s u j", u=2, j=2), vpool_b[:].indirect(offs_sb[:]), COPY)
@@ -98,25 +108,19 @@ def tile_attend_kv_append256_sink_kernel(tc, qT, kT, vT, new_kT, new_vT, vs, sin
 
         negsink = held.tile([P, 1], F32, name="negsink")
         nc.gpsimd.tensor_scalar(negsink[:], sink_sb[:], -1.0, 0.0, op0=MULT, op1=ADD)
-        vs_g = held.tile([P, N], F32, name="vs_g", tag="ring", align_bytes=64)
-        nc.vector.tensor_copy(vs_g[:], vs_sb[:].indirect(offs_sb[:]))
-        vs_ps = psum.tile([P, 4, P], F32, name="vs_ps")
-        for t in range(4):
-            nc.tensor.transpose(vs_ps[:, t, :], vs_g[:, t::4], ident_f[:])
 
         negm = held.tile([P, 1], F32, name="negm")
-        neg_score = held.tile([P, N], F32, name="neg_score")
-        nc.vector.tensor_scalar(neg_score[:], score[:], -1.0, negsink[:], op0=MULT, op1=MIN, accum_out=negm[:])
-        vs_col = held.tile([P, 4], F32, name="vs_col")
-        nc.vector.tensor_copy(vs_col[:], vs_ps[:, :, 0])
+        neg_score = held.tile([P, N], F32, name="neg_score", tag="neg_score", align_bytes=64)
+        negm_0 = held.tile([P, 1], F32, name="negm_0")
+        nc.vector.tensor_scalar(neg_score[:, : N // 2], score[0][:], -1.0, negsink[:], op0=MULT, op1=MIN, accum_out=negm_0[:])
+        nc.vector.tensor_scalar(neg_score[:, N // 2 :], score[1][:], -1.0, negm_0[:], op0=MULT, op1=MIN, accum_out=negm[:])
 
         p_sb = held.tile([P, 4, P], F32, name="p_sb")
         l_ab = held.tile([P, 2], F32, name="l_ab")
-        score_v = score[:].rearrange("q (s t) -> q t s", t=4)
         for h in range(2):
-            nc.scalar.activation(p_sb[:, 2 * h : 2 * h + 2, :], score_v[:, 2 * h : 2 * h + 2, :], EXP, bias=negm[:], accum_out=l_ab[:, h : h + 1])
+            nc.scalar.activation(p_sb[:, 2 * h : 2 * h + 2, :], score[h][:].rearrange("q (s t) -> q t s", t=2), EXP, bias=negm[:], accum_out=l_ab[:, h : h + 1])
 
-        v_c = held.tile([P, DV], U32, name="v_c", align_bytes=64)
+        v_c = held.tile([P, DV], U32, name="v_c", tag="neg_score", align_bytes=64)
         v_s = held.tile([P, DV], U8, name="v_s", align_bytes=64)
         nc.vector.quantize_mx(out=v_c[:].bitcast(FP8X4), scales=v_s[:], in_=v_b[:])
 

@@ -30,7 +30,7 @@ def tile_attend_kv_append256_sink_kernel(tc, qT, kT, vT, new_kT, new_vT, vs, sin
 
         slots_sb = held.tile([P, NEW // 16], U16, name="slots_sb")
         offs_sb = held.tile([P, N // 16], U16, name="offs_sb")
-        newv = held.tile([P, NEW], F32, name="newv", tag="ring", align_bytes=64)
+        newv = held.tile([P, NEW], F32, name="newv")
         vpool = held.tile([P, T], F32, name="vpool")
         newk01 = [held.tile([P, NEW], F32, name=f"newk{t}") for t in range(2)]
         newk23 = held.tile([P, 2, NEW], F32, name="newk23")
@@ -38,11 +38,11 @@ def tile_attend_kv_append256_sink_kernel(tc, qT, kT, vT, new_kT, new_vT, vs, sin
         kpool = [held.tile([P, T], F32, name=f"kpool{t}", tag=f"kpool{t}", align_bytes=64) for t in range(4)]
         q_raw = held.tile([P, 4, NQ], F32, name="q_raw")
         vs_sb = held.tile([P, T], F32, name="vs_sb")
-        sink_sb = held.tile([P, 1], F32, name="sink_sb")
+        sink_sb = held.tile([P, 1], F32, name="sink_sb", tag="ring", align_bytes=64)
 
         kT_v = kT.rearrange("(p t) n -> p t n", t=4)
         newk_v = new_kT.rearrange("(p t) n -> p t n", t=4)
-        nc.sync.dma_start(vs_sb[P - 1 : P, :], vs[0:1, :])
+        nc.scalar.dma_start(vs_sb[P - 1 : P, :], vs[0:1, :])
         nc.vector.memset(vs_sb[: P - 1, :], 0.0)
         nc.sync.dma_start(offs_sb[:], offs)
         for t in range(4):
@@ -53,9 +53,9 @@ def tile_attend_kv_append256_sink_kernel(tc, qT, kT, vT, new_kT, new_vT, vs, sin
                 nc.sync.dma_start(newk23[:], newk_v[:, 2:, :])
             if t == 0:
                 nc.sync.dma_start(slots_sb[:], slots)
+        nc.sync.dma_start(q_raw[:], qT.rearrange("b (p t) q -> p (b t) q", t=4))
         nc.sync.dma_start(newv[:], new_vT)
         nc.sync.dma_start(vpool[:], vT)
-        nc.sync.dma_start(q_raw[:], qT.rearrange("b (p t) q -> p (b t) q", t=4))
         nc.sync.dma_start(sink_sb[:], sink.rearrange("b q o -> (b q) o"))
 
         ident_f = held.tile([P, P], F32, name="ident_f")
@@ -83,11 +83,13 @@ def tile_attend_kv_append256_sink_kernel(tc, qT, kT, vT, new_kT, new_vT, vs, sin
         vpool_b = held.tile([P, T], BF16, name="vpool_b")
         nc.scalar.copy(vpool_b[:], vpool[:])
 
+        negsink = held.tile([P, 1], F32, name="negsink")
+        nc.gpsimd.tensor_scalar(negsink[:], sink_sb[:], -1.0, 0.0, op0=MULT, op1=ADD)
         k_g = held.tile([P, N * 4], BF16, name="k_g", tag="ring", align_bytes=64)
         k_g32 = k_g[:].bitcast(U32).rearrange("p (h s t u) -> p s h t u", h=2, t=2, u=2)
         for u in range(2):
             nc.vector.tensor_copy(k_g32[:, :, :, :, u], kpair[u][:].bitcast(U32).indirect(offs_sb[:]))
-        q_c = held.tile([P, NQ], U32, name="q_c", tag="kpair1", align_bytes=64)
+        q_c = held.tile([P, NQ], U32, name="q_c", tag="kpair0", align_bytes=64)
         q_s = held.tile([P, NQ], U8, name="q_s", align_bytes=64)
         nc.vector.quantize_mx(out=q_c[:].bitcast(FP8X4), scales=q_s[:], in_=q_b[:].rearrange("p q t -> p (q t)"))
         k_c = held.tile([P, N], U32, name="k_c", align_bytes=64)
@@ -98,16 +100,12 @@ def tile_attend_kv_append256_sink_kernel(tc, qT, kT, vT, new_kT, new_vT, vs, sin
             nc.vector.quantize_mx(out=k_c[:, c].bitcast(FP8X4), scales=k_s[:, c], in_=k_g[:, 2 * N * h : 2 * N * (h + 1)])
             nc.tensor.matmul_mx(score[h][:], lhsT=q_c[:].bitcast(FP8X4), lhsT_scale=q_s[:], rhs=k_c[:, c].bitcast(FP8X4), rhs_scale=k_s[:, c], start=True, stop=True)
 
-        v_g = held.tile([P, N], BF16, name="v_g", align_bytes=64)
+        v_g = held.tile([P, N], BF16, name="v_g", tag="kpool3", align_bytes=64)
         nc.scalar.activation(v_g[:].rearrange("p (u s j) -> p s u j", u=2, j=2), vpool_b[:].indirect(offs_sb[:]), COPY)
         v_ps = psum.tile([P, 2, DV], F32, name="v_ps")
         for u in range(2):
             nc.tensor.transpose(v_ps[:, u, :], v_g[:, u * (N // 2) : (u + 1) * (N // 2)].bitcast(F32), ident_f[:])
-        v_b = held.tile([P, DV * 4], BF16, name="v_b", align_bytes=64)
-        nc.scalar.copy(v_b[:].bitcast(F32).rearrange("p (e u) -> p e u", u=2), v_ps[:].rearrange("p u e -> p e u"))
 
-        negsink = held.tile([P, 1], F32, name="negsink")
-        nc.gpsimd.tensor_scalar(negsink[:], sink_sb[:], -1.0, 0.0, op0=MULT, op1=ADD)
 
         negm = held.tile([P, 1], F32, name="negm")
         neg_score = held.tile([P, N], F32, name="neg_score", tag="neg_score", align_bytes=64)
@@ -120,7 +118,9 @@ def tile_attend_kv_append256_sink_kernel(tc, qT, kT, vT, new_kT, new_vT, vs, sin
         for h in range(2):
             nc.scalar.activation(p_sb[:, 2 * h : 2 * h + 2, :], score[h][:].rearrange("q (s t) -> q t s", t=2), EXP, bias=negm[:], accum_out=l_ab[:, h : h + 1])
 
-        v_c = held.tile([P, DV], U32, name="v_c", tag="neg_score", align_bytes=64)
+        v_b = held.tile([P, DV * 4], BF16, name="v_b", tag="neg_score", align_bytes=64)
+        nc.vector.tensor_copy(v_b[:].bitcast(F32).rearrange("p (e u) -> p e u", u=2), v_ps[:].rearrange("p u e -> p e u"))
+        v_c = held.tile([P, DV], U32, name="v_c", align_bytes=64)
         v_s = held.tile([P, DV], U8, name="v_s", align_bytes=64)
         nc.vector.quantize_mx(out=v_c[:].bitcast(FP8X4), scales=v_s[:], in_=v_b[:])
 
@@ -146,7 +146,7 @@ def tile_attend_kv_append256_sink_kernel(tc, qT, kT, vT, new_kT, new_vT, vs, sin
         nc.tensor.matmul_mx(y_ps[:], lhsT=w_c[:].bitcast(FP8X4), lhsT_scale=w_s[:], rhs=v_c[:].bitcast(FP8X4), rhs_scale=v_s[:], start=True, stop=True)
 
         e_sink = held.tile([P, 1], F32, name="e_sink")
-        nc.scalar.activation(e_sink[:], sink_sb[:], EXP, bias=negm[:])
+        nc.scalar.activation(e_sink[:], negsink[:], EXP, bias=negm[:], scale=-1.0)
         l_0 = held.tile([P, 1], F32, name="l_0")
         nc.vector.scalar_tensor_tensor(l_0[:], l_ab[:, 0:1], e_sink[:], l_ab[:, 1:2], ADD, ADD)
         r_l = held.tile([P, 1], F32, name="r_l")

@@ -53,8 +53,8 @@ def tile_attend_kv_append256_sink_kernel(tc, qT, kT, vT, new_kT, new_vT, vs, sin
                 nc.sync.dma_start(newk23[:], newk_v[:, 2:, :])
             if t == 0:
                 nc.sync.dma_start(slots_sb[:], slots)
-        nc.sync.dma_start(q_raw[:], qT.rearrange("b (p t) q -> p (b t) q", t=4))
         nc.sync.dma_start(newv[:], new_vT)
+        nc.sync.dma_start(q_raw[:], qT.rearrange("b (p t) q -> p (b t) q", t=4))
         nc.sync.dma_start(vpool[:], vT)
         nc.sync.dma_start(sink_sb[:], sink.rearrange("b q o -> (b q) o"))
 
@@ -78,17 +78,26 @@ def tile_attend_kv_append256_sink_kernel(tc, qT, kT, vT, new_kT, new_vT, vs, sin
             nc.scalar.copy(kpair[t // 2][:].rearrange("p (n j) -> p n j", j=2)[:, :, t % 2], kpool[t][:])
 
         nc.vector.tensor_copy(vpool[:].indirect(slots_sb[:]), newv[:])
-        q_b = held.tile([P, NQ, 4], BF16, name="q_b", tag="kpool3", align_bytes=64)
+        q_b = held.tile([P, NQ, 4], BF16, name="q_b", tag="q_b", align_bytes=64)
         nc.scalar.copy(q_b[:], q_raw[:].rearrange("p t q -> p q t"))
         vpool_b = held.tile([P, T], BF16, name="vpool_b")
         nc.scalar.copy(vpool_b[:], vpool[:])
 
         negsink = held.tile([P, 1], F32, name="negsink")
         nc.gpsimd.tensor_scalar(negsink[:], sink_sb[:], -1.0, 0.0, op0=MULT, op1=ADD)
-        k_g = held.tile([P, N * 4], BF16, name="k_g", tag="ring", align_bytes=64)
-        k_g32 = k_g[:].bitcast(U32).rearrange("p (h s t u) -> p s h t u", h=2, t=2, u=2)
-        for u in range(2):
-            nc.vector.tensor_copy(k_g32[:, :, :, :, u], kpair[u][:].bitcast(U32).indirect(offs_sb[:]))
+        k_w = held.tile([P, 2 * N], U32, name="k_w", tag="ring", align_bytes=64)
+        k_g = [held.tile([P, N * 2], BF16, name=f"k_g{h}", align_bytes=64) for h in range(2)]
+        H = N // 2
+        for h, u, lo, hi in ((0, 0, 0, H), (0, 1, 0, H), (1, 0, 0, H), (1, 1, 0, H // 2), (1, 1, H // 2, H)):
+            nc.vector.tensor_copy(
+                k_w[:, (2 * h + u) * H + lo : (2 * h + u) * H + hi],
+                kpair[u][:].bitcast(U32).indirect(offs_sb[:, (h * H + lo) // 16 : (h * H + hi) // 16]),
+            )
+            if u == 1:
+                nc.scalar.copy(
+                    k_g[h][:].bitcast(U32).rearrange("p (n u) -> p n u", u=2)[:, lo:hi, :],
+                    k_w[:, h * N : (h + 1) * N].rearrange("p (u n) -> p n u", u=2)[:, lo:hi, :],
+                )
         q_c = held.tile([P, NQ], U32, name="q_c", tag="kpair0", align_bytes=64)
         q_s = held.tile([P, NQ], U8, name="q_s", align_bytes=64)
         nc.vector.quantize_mx(out=q_c[:].bitcast(FP8X4), scales=q_s[:], in_=q_b[:].rearrange("p q t -> p (q t)"))
@@ -97,10 +106,10 @@ def tile_attend_kv_append256_sink_kernel(tc, qT, kT, vT, new_kT, new_vT, vs, sin
         score = [psum.tile([P, N // 2], F32, name=f"score{h}") for h in range(2)]
         for h in range(2):
             c = slice(h * N // 2, (h + 1) * N // 2)
-            nc.vector.quantize_mx(out=k_c[:, c].bitcast(FP8X4), scales=k_s[:, c], in_=k_g[:, 2 * N * h : 2 * N * (h + 1)])
+            nc.vector.quantize_mx(out=k_c[:, c].bitcast(FP8X4), scales=k_s[:, c], in_=k_g[h][:])
             nc.tensor.matmul_mx(score[h][:], lhsT=q_c[:].bitcast(FP8X4), lhsT_scale=q_s[:], rhs=k_c[:, c].bitcast(FP8X4), rhs_scale=k_s[:, c], start=True, stop=True)
 
-        v_g = held.tile([P, N], BF16, name="v_g", tag="kpool3", align_bytes=64)
+        v_g = held.tile([P, N], BF16, name="v_g", tag="q_b", align_bytes=64)
         nc.scalar.activation(v_g[:].rearrange("p (u s j) -> p s u j", u=2, j=2), vpool_b[:].indirect(offs_sb[:]), COPY)
         v_ps = psum.tile([P, 2, DV], F32, name="v_ps")
         for u in range(2):
@@ -114,9 +123,16 @@ def tile_attend_kv_append256_sink_kernel(tc, qT, kT, vT, new_kT, new_vT, vs, sin
         nc.vector.tensor_scalar(neg_score[:, N // 2 :], score[1][:], -1.0, negm_0[:], op0=MULT, op1=MIN, accum_out=negm[:])
 
         p_sb = held.tile([P, 4, P], F32, name="p_sb")
-        l_ab = held.tile([P, 2], F32, name="l_ab")
-        for h in range(2):
-            nc.scalar.activation(p_sb[:, 2 * h : 2 * h + 2, :], score[h][:].rearrange("q (s t) -> q t s", t=2), EXP, bias=negm[:], accum_out=l_ab[:, h : h + 1])
+        l_ab = held.tile([P, 5], F32, name="l_ab")
+        for g in range(2):
+            for h in range(2):
+                nc.scalar.activation(
+                    p_sb[:, 2 * g : 2 * g + 2, h * P // 2 : (h + 1) * P // 2],
+                    score[h][:].rearrange("q (s t) -> q t s", t=4)[:, 2 * g : 2 * g + 2, :],
+                    EXP,
+                    bias=negm[:],
+                    accum_out=l_ab[:, 2 * g + h : 2 * g + h + 1],
+                )
 
         v_b = held.tile([P, DV * 4], BF16, name="v_b", tag="neg_score", align_bytes=64)
         nc.vector.tensor_copy(v_b[:].bitcast(F32).rearrange("p (e u) -> p e u", u=2), v_ps[:].rearrange("p u e -> p e u"))
@@ -145,10 +161,9 @@ def tile_attend_kv_append256_sink_kernel(tc, qT, kT, vT, new_kT, new_vT, vs, sin
         y_ps = psum.tile([P, DV], F32, name="y_ps")
         nc.tensor.matmul_mx(y_ps[:], lhsT=w_c[:].bitcast(FP8X4), lhsT_scale=w_s[:], rhs=v_c[:].bitcast(FP8X4), rhs_scale=v_s[:], start=True, stop=True)
 
-        e_sink = held.tile([P, 1], F32, name="e_sink")
-        nc.scalar.activation(e_sink[:], negsink[:], EXP, bias=negm[:], scale=-1.0)
+        nc.scalar.activation(l_ab[:, 4:5], negsink[:], EXP, bias=negm[:], scale=-1.0)
         l_0 = held.tile([P, 1], F32, name="l_0")
-        nc.vector.scalar_tensor_tensor(l_0[:], l_ab[:, 0:1], e_sink[:], l_ab[:, 1:2], ADD, ADD)
+        nc.vector.tensor_reduce(l_0[:], l_ab[:], AXIS_X, ADD)
         r_l = held.tile([P, 1], F32, name="r_l")
         nc.vector.reciprocal(r_l[:], l_0[:])
 

@@ -110,31 +110,24 @@ def tile_attend_kv_append256_sink_kernel(tc, qT, kT, vT, new_kT, new_vT, vs, sin
             nc.tensor.matmul_mx(score[h][:], lhsT=q_c[:].bitcast(FP8X4), lhsT_scale=q_s[:], rhs=k_c[:, c].bitcast(FP8X4), rhs_scale=k_s[:, c], start=True, stop=True)
 
         v_g = held.tile([P, N], BF16, name="v_g", tag="q_b", align_bytes=64)
-        nc.scalar.activation(v_g[:].rearrange("p (u s j) -> p s u j", u=2, j=2), vpool_b[:].indirect(offs_sb[:]), COPY)
+        nc.scalar.activation(v_g[:], vpool_b[:].indirect(offs_sb[:]), COPY)
         v_ps = psum.tile([P, 2, DV], F32, name="v_ps")
         for u in range(2):
-            nc.tensor.transpose(v_ps[:, u, :], v_g[:, u * (N // 2) : (u + 1) * (N // 2)].bitcast(F32), ident_f[:])
+            nc.tensor.transpose(v_ps[:, u, :], v_g[:].bitcast(F32)[:, u::2], ident_f[:])
 
 
         negm = held.tile([P, 1], F32, name="negm")
-        neg_score = held.tile([P, N], F32, name="neg_score", tag="neg_score", align_bytes=64)
-        negm_0 = held.tile([P, 1], F32, name="negm_0")
-        nc.vector.tensor_scalar(neg_score[:, : N // 2], score[0][:], -1.0, negsink[:], op0=MULT, op1=MIN, accum_out=negm_0[:])
-        nc.vector.tensor_scalar(neg_score[:, N // 2 :], score[1][:], -1.0, negm_0[:], op0=MULT, op1=MIN, accum_out=negm[:])
+        neg_score = held.tile([P, 4, P], F32, name="neg_score")
+        negm_0 = held.tile([P, 1], F32, name="negm_0", tag="v_b", align_bytes=64)
+        nc.vector.tensor_scalar(neg_score[:, :, : P // 2], score[0][:].rearrange("q (s t) -> q t s", t=4), -1.0, negsink[:], op0=MULT, op1=MIN, accum_out=negm_0[:])
+        nc.vector.tensor_scalar(neg_score[:, :, P // 2 :], score[1][:].rearrange("q (s t) -> q t s", t=4), -1.0, negm_0[:], op0=MULT, op1=MIN, accum_out=negm[:])
 
         p_sb = held.tile([P, 4, P], F32, name="p_sb")
         l_ab = held.tile([P, 5], F32, name="l_ab")
-        for g in range(2):
-            for h in range(2):
-                nc.scalar.activation(
-                    p_sb[:, 2 * g : 2 * g + 2, h * P // 2 : (h + 1) * P // 2],
-                    score[h][:].rearrange("q (s t) -> q t s", t=4)[:, 2 * g : 2 * g + 2, :],
-                    EXP,
-                    bias=negm[:],
-                    accum_out=l_ab[:, 2 * g + h : 2 * g + h + 1],
-                )
+        for t in range(4):
+            nc.scalar.activation(p_sb[:, t, :], neg_score[:, t, :], EXP, bias=negm[:], scale=-1.0, accum_out=l_ab[:, t : t + 1])
 
-        v_b = held.tile([P, DV * 4], BF16, name="v_b", tag="neg_score", align_bytes=64)
+        v_b = held.tile([P, DV * 4], BF16, name="v_b", tag="v_b", align_bytes=64)
         nc.vector.tensor_copy(v_b[:].bitcast(F32).rearrange("p (e u) -> p e u", u=2), v_ps[:].rearrange("p u e -> p e u"))
         v_c = held.tile([P, DV], U32, name="v_c", align_bytes=64)
         v_s = held.tile([P, DV], U8, name="v_s", align_bytes=64)

@@ -32,9 +32,7 @@ def tile_attend_kv_append256_sink_kernel(tc, qT, kT, vT, new_kT, new_vT, vs, sin
         offs_sb = held.tile([P, N // 16], U16, name="offs_sb")
         newv = held.tile([P, NEW], F32, name="newv")
         vpool = held.tile([P, T], F32, name="vpool")
-        newk01 = [held.tile([P, NEW], F32, name=f"newk{t}") for t in range(2)]
-        newk23 = held.tile([P, 2, NEW], F32, name="newk23")
-        newk = [newk01[0][:], newk01[1][:], newk23[:, 0, :], newk23[:, 1, :]]
+        newk = [held.tile([P, NEW], F32, name=f"newk{t}")[:] for t in range(4)]
         kpool = [held.tile([P, T], F32, name=f"kpool{t}", tag=f"kpool{t}", align_bytes=64) for t in range(4)]
         q_raw = held.tile([P, 4, NQ], F32, name="q_raw")
         vs_sb = held.tile([P, T], F32, name="vs_sb")
@@ -47,16 +45,13 @@ def tile_attend_kv_append256_sink_kernel(tc, qT, kT, vT, new_kT, new_vT, vs, sin
         nc.sync.dma_start(offs_sb[:], offs)
         for t in range(4):
             nc.sync.dma_start(kpool[t][:], kT_v[:, t, :])
-            if t < 2:
-                nc.sync.dma_start(newk[t], newk_v[:, t, :])
-            if t == 2:
-                nc.sync.dma_start(newk23[:], newk_v[:, 2:, :])
+            nc.sync.dma_start(newk[t], newk_v[:, t, :])
             if t == 0:
                 nc.sync.dma_start(slots_sb[:], slots)
         nc.sync.dma_start(newv[:], new_vT)
-        nc.sync.dma_start(q_raw[:], qT.rearrange("b (p t) q -> p (b t) q", t=4))
         nc.sync.dma_start(vpool[:], vT)
         nc.sync.dma_start(sink_sb[:], sink.rearrange("b q o -> (b q) o"))
+        nc.sync.dma_start(q_raw[:], qT.rearrange("b (p t) q -> p (b t) q", t=4))
 
         ident_f = held.tile([P, P], F32, name="ident_f")
         make_identity(nc, ident_f[:])
@@ -79,7 +74,7 @@ def tile_attend_kv_append256_sink_kernel(tc, qT, kT, vT, new_kT, new_vT, vs, sin
 
         nc.vector.tensor_copy(vpool[:].indirect(slots_sb[:]), newv[:])
         q_b = held.tile([P, NQ, 4], BF16, name="q_b", tag="q_b", align_bytes=64)
-        nc.scalar.copy(q_b[:], q_raw[:].rearrange("p t q -> p q t"))
+        nc.gpsimd.tensor_scalar(q_b[:], q_raw[:].rearrange("p t q -> p q t"), 1.0, 0.0, op0=MULT, op1=ADD)
         vpool_b = held.tile([P, T], BF16, name="vpool_b")
         nc.scalar.copy(vpool_b[:], vpool[:])
 

@@ -73,42 +73,52 @@ def tile_attend_kv_append256_sink_kernel(tc, qT, kT, vT, new_kT, new_vT, vs, sin
             nc.scalar.copy(kpair[t // 2][:].rearrange("p (n j) -> p n j", j=2)[:, :, t % 2], kpool[t][:])
 
         nc.vector.tensor_copy(vpool[:].indirect(slots_sb[:]), newv[:])
-        q_b = held.tile([P, NQ, 4], BF16, name="q_b", tag="q_b", align_bytes=64)
-        nc.gpsimd.tensor_scalar(q_b[:], q_raw[:].rearrange("p t q -> p q t"), 1.0, 0.0, op0=MULT, op1=ADD)
+        v_q = held.tile([P, N + N // 4], BF16, name="v_q", align_bytes=64)
+        q_b = v_q[:, N // 4 :]
+        nc.gpsimd.tensor_scalar(q_b.rearrange("p (q t) -> p q t", t=4), q_raw[:].rearrange("p t q -> p q t"), 1.0, 0.0, op0=MULT, op1=ADD)
         vpool_b = held.tile([P, T], BF16, name="vpool_b")
         nc.scalar.copy(vpool_b[:], vpool[:])
 
         negsink = held.tile([P, 1], F32, name="negsink")
         nc.gpsimd.tensor_scalar(negsink[:], sink_sb[:], -1.0, 0.0, op0=MULT, op1=ADD)
         k_w = held.tile([P, 2 * N], U32, name="k_w", tag="ring", align_bytes=64)
-        k_g = [held.tile([P, N * 2], BF16, name=f"k_g{h}", align_bytes=64) for h in range(2)]
-        H = N // 2
-        for h, u, lo, hi in ((0, 0, 0, H), (0, 1, 0, H), (1, 0, 0, H), (1, 1, 0, H // 2), (1, 1, H // 2, H)):
-            nc.vector.tensor_copy(
-                k_w[:, (2 * h + u) * H + lo : (2 * h + u) * H + hi],
-                kpair[u][:].bitcast(U32).indirect(offs_sb[:, (h * H + lo) // 16 : (h * H + hi) // 16]),
-            )
-            if u == 1:
-                nc.scalar.copy(
-                    k_g[h][:].bitcast(U32).rearrange("p (n u) -> p n u", u=2)[:, lo:hi, :],
-                    k_w[:, h * N : (h + 1) * N].rearrange("p (u n) -> p n u", u=2)[:, lo:hi, :],
-                )
+        H, Q = N // 2, N // 4
+        k_a = held.tile([P, H * 4], BF16, name="k_a", align_bytes=64)
+        k_b = held.tile([P, Q * 4], BF16, name="k_b", align_bytes=64)
+        k_last = k_w[:, : 2 * Q].rearrange("p (n u) -> p n u", u=2)
+
+        def gather(dst, u, lo, hi):
+            nc.vector.tensor_copy(dst, kpair[u][:].bitcast(U32).indirect(offs_sb[:, lo // 16 : hi // 16]))
+
+        gather(k_w[:, :H], 0, 0, H)
+        gather(k_w[:, H:N], 1, 0, H)
+        nc.scalar.copy(k_a[:].bitcast(U32).rearrange("p (n u) -> p n u", u=2), k_w[:, :N].rearrange("p (u n) -> p n u", u=2))
+        nc.scalar.activation(v_q[:, :Q], vpool_b[:].indirect(offs_sb[:, : Q // 16]), COPY)
+        gather(k_w[:, N : N + H], 0, H, N)
+        gather(k_w[:, N + H : N + H + Q], 1, H, H + Q)
+        nc.scalar.copy(k_b[:].bitcast(U32).rearrange("p (n u) -> p n u", u=2), k_w[:, N:].rearrange("p (u n) -> p n u", u=2)[:, :Q, :])
+        nc.scalar.copy(k_last[:, :, 0], k_w[:, N + Q : N + H])
+
         q_c = held.tile([P, NQ], U32, name="q_c", tag="kpair0", align_bytes=64)
         q_s = held.tile([P, NQ], U8, name="q_s", align_bytes=64)
-        nc.vector.quantize_mx(out=q_c[:].bitcast(FP8X4), scales=q_s[:], in_=q_b[:].rearrange("p q t -> p (q t)"))
+        nc.vector.quantize_mx(out=q_c[:].bitcast(FP8X4), scales=q_s[:], in_=q_b)
         k_c = held.tile([P, N], U32, name="k_c", align_bytes=64)
         k_s = held.tile([P, N], U8, name="k_s", align_bytes=64)
-        score = [psum.tile([P, N // 2], F32, name=f"score{h}") for h in range(2)]
-        for h in range(2):
-            c = slice(h * N // 2, (h + 1) * N // 2)
-            nc.vector.quantize_mx(out=k_c[:, c].bitcast(FP8X4), scales=k_s[:, c], in_=k_g[h][:])
-            nc.tensor.matmul_mx(score[h][:], lhsT=q_c[:].bitcast(FP8X4), lhsT_scale=q_s[:], rhs=k_c[:, c].bitcast(FP8X4), rhs_scale=k_s[:, c], start=True, stop=True)
+        score = [psum.tile([P, H], F32, name=f"score{h}") for h in range(2)]
 
-        v_g = held.tile([P, N], BF16, name="v_g", tag="q_b", align_bytes=64)
-        nc.scalar.activation(v_g[:], vpool_b[:].indirect(offs_sb[:]), COPY)
+        def scores(dst, src, lo, hi):
+            nc.vector.quantize_mx(out=k_c[:, lo:hi].bitcast(FP8X4), scales=k_s[:, lo:hi], in_=src)
+            nc.tensor.matmul_mx(dst, lhsT=q_c[:].bitcast(FP8X4), lhsT_scale=q_s[:], rhs=k_c[:, lo:hi].bitcast(FP8X4), rhs_scale=k_s[:, lo:hi], start=True, stop=True)
+
+        scores(score[0][:], k_a[:], 0, H)
+        gather(k_last[:, :, 1], 1, H + Q, N)
+        scores(score[1][:, :Q], k_b[:], H, H + Q)
+        scores(score[1][:, Q:], k_w[:, : 2 * Q].bitcast(BF16), H + Q, N)
+
+        nc.scalar.activation(v_q[:, Q:N], vpool_b[:].indirect(offs_sb[:, Q // 16 :]), COPY)
         v_ps = psum.tile([P, 2, DV], F32, name="v_ps")
         for u in range(2):
-            nc.tensor.transpose(v_ps[:, u, :], v_g[:].bitcast(F32)[:, u::2], ident_f[:])
+            nc.tensor.transpose(v_ps[:, u, :], v_q[:, :N].bitcast(F32)[:, u::2], ident_f[:])
 
 
         negm = held.tile([P, 1], F32, name="negm")

@@ -55,9 +55,6 @@ def tile_attend_kv_append256_sink_kernel(tc, qT, kT, vT, new_kT, new_vT, vs, sin
 
         ident_f = held.tile([P, P], F32, name="ident_f")
         make_identity(nc, ident_f[:])
-        warm = held.tile([P, 1], F32, name="warm")
-        nc.gpsimd.memset(warm[:], 0.0)
-        nc.scalar.activation(warm[:], warm[:], EXP)
 
         vs_g = held.tile([P, N], F32, name="vs_g", align_bytes=64)
         nc.vector.tensor_copy(vs_g[:], vs_sb[:].indirect(offs_sb[:]))

@@ -6,6 +6,7 @@ from concourse.masks import make_identity
 F32 = mybir.dt.float32
 BF16 = mybir.dt.bfloat16
 U32 = mybir.dt.uint32
+I32 = mybir.dt.int32
 U16 = mybir.dt.uint16
 U8 = mybir.dt.uint8
 FP8X4 = mybir.dt.float8_e4m3fn_x4
@@ -19,6 +20,7 @@ AXIS_X = mybir.AxisListType.X
 
 P = 128
 N, T, D, DV, NQ, NEW = 512, 1024, 512, 128, 128, 256
+SPLIT = (512, 0, 0, 0)
 FLOPS = 2 * NQ * N * (D + DV)
 
 
@@ -34,7 +36,7 @@ def tile_attend_kv_append256_sink_kernel(tc, qT, kT, vT, new_kT, new_vT, vs, sin
         vpool = held.tile([P, T], F32, name="vpool")
         newk = [held.tile([P, NEW], F32, name=f"newk{t}")[:] for t in range(4)]
         kpool = [held.tile([P, T], F32, name=f"kpool{t}", tag=f"kpool{t}", align_bytes=64) for t in range(4)]
-        q_raw = held.tile([P, 4, NQ], F32, name="q_raw")
+        q_raw = held.tile([P, 4, NQ], F32, name="q_raw", tag="q_raw", align_bytes=64)
         vs_sb = held.tile([P, T], F32, name="vs_sb")
         sink_sb = held.tile([P, 1], F32, name="sink_sb", tag="ring", align_bytes=64)
 
@@ -64,58 +66,55 @@ def tile_attend_kv_append256_sink_kernel(tc, qT, kT, vT, new_kT, new_vT, vs, sin
         vs_col = held.tile([P, 4], F32, name="vs_col")
         nc.scalar.copy(vs_col[:], vs_ps[:, :, P - 1])
 
-        kpair = [held.tile([P, 2 * T], BF16, name=f"kpair{u}", tag=f"kpair{u}", align_bytes=64) for u in range(2)]
+        H = N // 2
+        kb = [held.tile([P, T], BF16, name=f"kb{t}") for t in range(4)]
+        k_w = held.tile([P, 4 * N], BF16, name="k_w", align_bytes=64)
+        k_wv = k_w[:].rearrange("p (h u n j) -> p h u n j", h=2, u=2, j=2)
         for t in range(4):
+            split = SPLIT[t]
             nc.vector.tensor_copy(kpool[t][:].indirect(slots_sb[:]), newk[t])
-            nc.scalar.copy(kpair[t // 2][:].rearrange("p (n j) -> p n j", j=2)[:, :, t % 2], kpool[t][:])
+            if split:
+                nc.scalar.copy(kb[t][:, :split], kpool[t][:, :split])
+            nc.gpsimd.tensor_scalar(kb[t][:, split:], kpool[t][:, split:], 1.0, 0.0, op0=MULT, op1=ADD)
+            if t < 3:
+                nc.scalar.activation(k_wv[:, :, t // 2, :, t % 2], kb[t][:].indirect(offs_sb[:]), COPY)
+            else:
+                for h in range(2):
+                    nc.scalar.activation(k_wv[:, h, t // 2, :, t % 2], kb[t][:].indirect(offs_sb[:, h * H // 16 : (h + 1) * H // 16]), COPY)
 
         nc.vector.tensor_copy(vpool[:].indirect(slots_sb[:]), newv[:])
-        v_q = held.tile([P, N + N // 4], BF16, name="v_q", align_bytes=64)
-        q_b = v_q[:, N // 4 :]
-        nc.gpsimd.tensor_scalar(q_b.rearrange("p (q t) -> p q t", t=4), q_raw[:].rearrange("p t q -> p q t"), 1.0, 0.0, op0=MULT, op1=ADD)
-        vpool_b = held.tile([P, T], BF16, name="vpool_b")
-        nc.scalar.copy(vpool_b[:], vpool[:])
-
         negsink = held.tile([P, 1], F32, name="negsink")
         nc.gpsimd.tensor_scalar(negsink[:], sink_sb[:], -1.0, 0.0, op0=MULT, op1=ADD)
-        k_w = held.tile([P, 2 * N], U32, name="k_w", tag="ring", align_bytes=64)
-        H, Q = N // 2, N // 4
-        k_a = held.tile([P, H * 4], BF16, name="k_a", align_bytes=64)
-        k_b = held.tile([P, Q * 4], BF16, name="k_b", align_bytes=64)
-        k_last = k_w[:, : 2 * Q].rearrange("p (n u) -> p n u", u=2)
+        q_b = held.tile([P, N], BF16, name="q_b", align_bytes=64)
+        nc.gpsimd.tensor_scalar(q_b[:].rearrange("p (q t) -> p q t", t=4), q_raw[:].rearrange("p t q -> p q t"), 1.0, 0.0, op0=MULT, op1=ADD)
+        vpool_b = held.tile([P, T], BF16, name="vpool_b", tag="ring", align_bytes=64)
+        nc.scalar.copy(vpool_b[:], vpool[:])
+        v_q = held.tile([P, N], BF16, name="v_q", align_bytes=64)
+        nc.scalar.activation(v_q[:], vpool_b[:].indirect(offs_sb[:]), COPY)
 
-        def gather(dst, u, lo, hi):
-            nc.vector.tensor_copy(dst, kpair[u][:].bitcast(U32).indirect(offs_sb[:, lo // 16 : hi // 16]))
-
-        gather(k_w[:, :H], 0, 0, H)
-        gather(k_w[:, H:N], 1, 0, H)
-        nc.scalar.copy(k_a[:].bitcast(U32).rearrange("p (n u) -> p n u", u=2), k_w[:, :N].rearrange("p (u n) -> p n u", u=2))
-        nc.scalar.activation(v_q[:, :Q], vpool_b[:].indirect(offs_sb[:, : Q // 16]), COPY)
-        gather(k_w[:, N : N + H], 0, H, N)
-        gather(k_w[:, N + H : N + H + Q], 1, H, H + Q)
-        nc.scalar.copy(k_b[:].bitcast(U32).rearrange("p (n u) -> p n u", u=2), k_w[:, N:].rearrange("p (u n) -> p n u", u=2)[:, :Q, :])
-        nc.scalar.copy(k_last[:, :, 0], k_w[:, N + Q : N + H])
-
-        q_c = held.tile([P, NQ], U32, name="q_c", tag="kpair0", align_bytes=64)
+        k_in = held.tile([P, 4 * N], BF16, name="k_in", tag="q_raw", align_bytes=64)
+        q_c = held.tile([P, NQ], U32, name="q_c", align_bytes=64)
         q_s = held.tile([P, NQ], U8, name="q_s", align_bytes=64)
-        nc.vector.quantize_mx(out=q_c[:].bitcast(FP8X4), scales=q_s[:], in_=q_b)
         k_c = held.tile([P, N], U32, name="k_c", align_bytes=64)
         k_s = held.tile([P, N], U8, name="k_s", align_bytes=64)
-        score = [psum.tile([P, H], F32, name=f"score{h}") for h in range(2)]
+        score = [psum.tile([P, H], F32, name=f"score{h}", tag=f"score{h}") for h in range(2)]
 
-        def scores(dst, src, lo, hi):
-            nc.vector.quantize_mx(out=k_c[:, lo:hi].bitcast(FP8X4), scales=k_s[:, lo:hi], in_=src)
-            nc.tensor.matmul_mx(dst, lhsT=q_c[:].bitcast(FP8X4), lhsT_scale=q_s[:], rhs=k_c[:, lo:hi].bitcast(FP8X4), rhs_scale=k_s[:, lo:hi], start=True, stop=True)
+        def weave(h):
+            nc.vector.tensor_copy(
+                k_in[:, h * 4 * H : (h + 1) * 4 * H].bitcast(I32).rearrange("p (n u) -> p n u", u=2),
+                k_w[:, h * 4 * H : (h + 1) * 4 * H].bitcast(I32).rearrange("p (u n) -> p n u", u=2),
+            )
 
-        scores(score[0][:], k_a[:], 0, H)
-        gather(k_last[:, :, 1], 1, H + Q, N)
-        scores(score[1][:, :Q], k_b[:], H, H + Q)
-        scores(score[1][:, Q:], k_w[:, : 2 * Q].bitcast(BF16), H + Q, N)
+        def scores(h):
+            c = slice(h * H, (h + 1) * H)
+            nc.vector.quantize_mx(out=k_c[:, c].bitcast(FP8X4), scales=k_s[:, c], in_=k_in[:, h * 4 * H : (h + 1) * 4 * H])
+            nc.tensor.matmul_mx(score[h][:], lhsT=q_c[:].bitcast(FP8X4), lhsT_scale=q_s[:], rhs=k_c[:, c].bitcast(FP8X4), rhs_scale=k_s[:, c], start=True, stop=True)
 
-        nc.scalar.activation(v_q[:, Q:N], vpool_b[:].indirect(offs_sb[:, Q // 16 :]), COPY)
-        v_ps = psum.tile([P, 2, DV], F32, name="v_ps")
-        for u in range(2):
-            nc.tensor.transpose(v_ps[:, u, :], v_q[:, :N].bitcast(F32)[:, u::2], ident_f[:])
+        weave(0)
+        nc.vector.quantize_mx(out=q_c[:].bitcast(FP8X4), scales=q_s[:], in_=q_b[:])
+        weave(1)
+        scores(0)
+        scores(1)
 
 
         negm = held.tile([P, 1], F32, name="negm")
@@ -123,6 +122,10 @@ def tile_attend_kv_append256_sink_kernel(tc, qT, kT, vT, new_kT, new_vT, vs, sin
         negm_0 = held.tile([P, 1], F32, name="negm_0", tag="v_b", align_bytes=64)
         nc.vector.tensor_scalar(neg_score[:, :, : P // 2], score[0][:].rearrange("q (s t) -> q t s", t=4), -1.0, negsink[:], op0=MULT, op1=MIN, accum_out=negm_0[:])
         nc.vector.tensor_scalar(neg_score[:, :, P // 2 :], score[1][:].rearrange("q (s t) -> q t s", t=4), -1.0, negm_0[:], op0=MULT, op1=MIN, accum_out=negm[:])
+
+        v_ps = psum.tile([P, 2, DV], F32, name="v_ps", tag="score0")
+        for u in range(2):
+            nc.tensor.transpose(v_ps[:, u, :], v_q[:].bitcast(F32)[:, u::2], ident_f[:])
 
         p_sb = held.tile([P, 4, P], F32, name="p_sb")
         l_ab = held.tile([P, 5], F32, name="l_ab")

@@ -67,9 +67,9 @@ def tile_attend_kv_append256_sink_kernel(tc, qT, kT, vT, new_kT, new_vT, vs, sin
         nc.scalar.copy(vs_col[:], vs_ps[:, :, P - 1])
 
         H = N // 2
-        kb = [held.tile([P, T], BF16, name=f"kb{t}") for t in range(4)]
-        k_w = held.tile([P, 4 * N], BF16, name="k_w", align_bytes=64)
-        k_wv = k_w[:].rearrange("p (h u n j) -> p h u n j", h=2, u=2, j=2)
+        kb = [held.tile([P, T], BF16, name=f"kb{t}", tag=f"kb{t}", align_bytes=64) for t in range(4)]
+        k_in = held.tile([P, 4 * N], BF16, name="k_in", align_bytes=64)
+        k_v = k_in[:].rearrange("p (n t) -> p n t", t=4)
         for t in range(4):
             split = SPLIT[t]
             nc.vector.tensor_copy(kpool[t][:].indirect(slots_sb[:]), newk[t])
@@ -77,42 +77,31 @@ def tile_attend_kv_append256_sink_kernel(tc, qT, kT, vT, new_kT, new_vT, vs, sin
                 nc.scalar.copy(kb[t][:, :split], kpool[t][:, :split])
             nc.gpsimd.tensor_scalar(kb[t][:, split:], kpool[t][:, split:], 1.0, 0.0, op0=MULT, op1=ADD)
             if t < 3:
-                nc.scalar.activation(k_wv[:, :, t // 2, :, t % 2], kb[t][:].indirect(offs_sb[:]), COPY)
+                nc.scalar.activation(k_v[:, :, t], kb[t][:].indirect(offs_sb[:]), COPY)
             else:
                 for h in range(2):
-                    nc.scalar.activation(k_wv[:, h, t // 2, :, t % 2], kb[t][:].indirect(offs_sb[:, h * H // 16 : (h + 1) * H // 16]), COPY)
+                    nc.scalar.activation(k_v[:, h * H : (h + 1) * H, t], kb[t][:].indirect(offs_sb[:, h * H // 16 : (h + 1) * H // 16]), COPY)
 
         nc.vector.tensor_copy(vpool[:].indirect(slots_sb[:]), newv[:])
+        v_q = held.tile([P, N], BF16, name="v_q", align_bytes=64)
+        nc.vector.tensor_copy(v_q[:], vpool[:].indirect(offs_sb[:]))
         negsink = held.tile([P, 1], F32, name="negsink")
         nc.gpsimd.tensor_scalar(negsink[:], sink_sb[:], -1.0, 0.0, op0=MULT, op1=ADD)
         q_b = held.tile([P, N], BF16, name="q_b", align_bytes=64)
         nc.gpsimd.tensor_scalar(q_b[:].rearrange("p (q t) -> p q t", t=4), q_raw[:].rearrange("p t q -> p q t"), 1.0, 0.0, op0=MULT, op1=ADD)
-        vpool_b = held.tile([P, T], BF16, name="vpool_b", tag="ring", align_bytes=64)
-        nc.scalar.copy(vpool_b[:], vpool[:])
-        v_q = held.tile([P, N], BF16, name="v_q", align_bytes=64)
-        nc.scalar.activation(v_q[:], vpool_b[:].indirect(offs_sb[:]), COPY)
 
-        k_in = held.tile([P, 4 * N], BF16, name="k_in", tag="q_raw", align_bytes=64)
         q_c = held.tile([P, NQ], U32, name="q_c", align_bytes=64)
         q_s = held.tile([P, NQ], U8, name="q_s", align_bytes=64)
-        k_c = held.tile([P, N], U32, name="k_c", align_bytes=64)
+        k_c = held.tile([P, N], U32, name="k_c", tag="q_raw", align_bytes=64)
         k_s = held.tile([P, N], U8, name="k_s", align_bytes=64)
         score = [psum.tile([P, H], F32, name=f"score{h}", tag=f"score{h}") for h in range(2)]
-
-        def weave(h):
-            nc.vector.tensor_copy(
-                k_in[:, h * 4 * H : (h + 1) * 4 * H].bitcast(I32).rearrange("p (n u) -> p n u", u=2),
-                k_w[:, h * 4 * H : (h + 1) * 4 * H].bitcast(I32).rearrange("p (u n) -> p n u", u=2),
-            )
 
         def scores(h):
             c = slice(h * H, (h + 1) * H)
             nc.vector.quantize_mx(out=k_c[:, c].bitcast(FP8X4), scales=k_s[:, c], in_=k_in[:, h * 4 * H : (h + 1) * 4 * H])
             nc.tensor.matmul_mx(score[h][:], lhsT=q_c[:].bitcast(FP8X4), lhsT_scale=q_s[:], rhs=k_c[:, c].bitcast(FP8X4), rhs_scale=k_s[:, c], start=True, stop=True)
 
-        weave(0)
         nc.vector.quantize_mx(out=q_c[:].bitcast(FP8X4), scales=q_s[:], in_=q_b[:])
-        weave(1)
         scores(0)
         scores(1)
 
@@ -126,14 +115,14 @@ def tile_attend_kv_append256_sink_kernel(tc, qT, kT, vT, new_kT, new_vT, vs, sin
         v_ps = psum.tile([P, 2, DV], F32, name="v_ps", tag="score0")
         for u in range(2):
             nc.tensor.transpose(v_ps[:, u, :], v_q[:].bitcast(F32)[:, u::2], ident_f[:])
+        v_b = held.tile([P, DV * 4], BF16, name="v_b", tag="v_b", align_bytes=64)
+        nc.vector.tensor_copy(v_b[:].bitcast(F32).rearrange("p (e u) -> p e u", u=2), v_ps[:].rearrange("p u e -> p e u"))
 
         p_sb = held.tile([P, 4, P], F32, name="p_sb")
         l_ab = held.tile([P, 5], F32, name="l_ab")
         for t in range(4):
             nc.scalar.activation(p_sb[:, t, :], neg_score[:, t, :], EXP, bias=negm[:], scale=-1.0, accum_out=l_ab[:, t : t + 1])
 
-        v_b = held.tile([P, DV * 4], BF16, name="v_b", tag="v_b", align_bytes=64)
-        nc.vector.tensor_copy(v_b[:].bitcast(F32).rearrange("p (e u) -> p e u", u=2), v_ps[:].rearrange("p u e -> p e u"))
         v_c = held.tile([P, DV], U32, name="v_c", align_bytes=64)
         v_s = held.tile([P, DV], U8, name="v_s", align_bytes=64)
         nc.vector.quantize_mx(out=v_c[:].bitcast(FP8X4), scales=v_s[:], in_=v_b[:])

@@ -68,8 +68,12 @@ def tile_attend_kv_append256_sink_kernel(tc, qT, kT, vT, new_kT, new_vT, vs, sin
 
         H = N // 2
         kb = [held.tile([P, T], BF16, name=f"kb{t}", tag=f"kb{t}", align_bytes=64) for t in range(4)]
-        k_in = held.tile([P, 4 * N], BF16, name="k_in", align_bytes=64)
-        k_v = k_in[:].rearrange("p (n t) -> p n t", t=4)
+        Q = N // 4
+        stage = held.tile([P, 4 * N + 2 * N - 2 * Q], BF16, name="stage", align_bytes=64)
+        k_in = stage[:, : 4 * N]
+        v_q = stage[:, 4 * N - Q : 5 * N - Q]
+        q_b = stage[:, 5 * N - 2 * Q :]
+        k_v = k_in.rearrange("p (n t) -> p n t", t=4)
         for t in range(4):
             split = SPLIT[t]
             nc.vector.tensor_copy(kpool[t][:].indirect(slots_sb[:]), newk[t])
@@ -83,12 +87,14 @@ def tile_attend_kv_append256_sink_kernel(tc, qT, kT, vT, new_kT, new_vT, vs, sin
                     nc.scalar.activation(k_v[:, h * H : (h + 1) * H, t], kb[t][:].indirect(offs_sb[:, h * H // 16 : (h + 1) * H // 16]), COPY)
 
         nc.vector.tensor_copy(vpool[:].indirect(slots_sb[:]), newv[:])
-        v_q = held.tile([P, N], BF16, name="v_q", align_bytes=64)
-        nc.vector.tensor_copy(v_q[:], vpool[:].indirect(offs_sb[:]))
+
+        def gather_v(lo, hi):
+            nc.vector.tensor_copy(v_q[:, lo:hi], vpool[:].indirect(offs_sb[:, lo // 16 : hi // 16]))
+
+        gather_v(Q, 3 * Q)
         negsink = held.tile([P, 1], F32, name="negsink")
         nc.gpsimd.tensor_scalar(negsink[:], sink_sb[:], -1.0, 0.0, op0=MULT, op1=ADD)
-        q_b = held.tile([P, N], BF16, name="q_b", align_bytes=64)
-        nc.gpsimd.tensor_scalar(q_b[:].rearrange("p (q t) -> p q t", t=4), q_raw[:].rearrange("p t q -> p q t"), 1.0, 0.0, op0=MULT, op1=ADD)
+        nc.gpsimd.tensor_scalar(q_b.rearrange("p (q t) -> p q t", t=4), q_raw[:].rearrange("p t q -> p q t"), 1.0, 0.0, op0=MULT, op1=ADD)
 
         q_c = held.tile([P, NQ], U32, name="q_c", align_bytes=64)
         q_s = held.tile([P, NQ], U8, name="q_s", align_bytes=64)
@@ -101,8 +107,9 @@ def tile_attend_kv_append256_sink_kernel(tc, qT, kT, vT, new_kT, new_vT, vs, sin
             nc.vector.quantize_mx(out=k_c[:, c].bitcast(FP8X4), scales=k_s[:, c], in_=k_in[:, h * 4 * H : (h + 1) * 4 * H])
             nc.tensor.matmul_mx(score[h][:], lhsT=q_c[:].bitcast(FP8X4), lhsT_scale=q_s[:], rhs=k_c[:, c].bitcast(FP8X4), rhs_scale=k_s[:, c], start=True, stop=True)
 
-        nc.vector.quantize_mx(out=q_c[:].bitcast(FP8X4), scales=q_s[:], in_=q_b[:])
+        nc.vector.quantize_mx(out=q_c[:].bitcast(FP8X4), scales=q_s[:], in_=q_b)
         scores(0)
+        gather_v(3 * Q, N)
         scores(1)
 
 
@@ -110,11 +117,12 @@ def tile_attend_kv_append256_sink_kernel(tc, qT, kT, vT, new_kT, new_vT, vs, sin
         neg_score = held.tile([P, 4, P], F32, name="neg_score")
         negm_0 = held.tile([P, 1], F32, name="negm_0", tag="v_b", align_bytes=64)
         nc.vector.tensor_scalar(neg_score[:, :, : P // 2], score[0][:].rearrange("q (s t) -> q t s", t=4), -1.0, negsink[:], op0=MULT, op1=MIN, accum_out=negm_0[:])
+        gather_v(0, Q)
         nc.vector.tensor_scalar(neg_score[:, :, P // 2 :], score[1][:].rearrange("q (s t) -> q t s", t=4), -1.0, negm_0[:], op0=MULT, op1=MIN, accum_out=negm[:])
 
         v_ps = psum.tile([P, 2, DV], F32, name="v_ps", tag="score0")
         for u in range(2):
-            nc.tensor.transpose(v_ps[:, u, :], v_q[:].bitcast(F32)[:, u::2], ident_f[:])
+            nc.tensor.transpose(v_ps[:, u, :], v_q.bitcast(F32)[:, u::2], ident_f[:])
         v_b = held.tile([P, DV * 4], BF16, name="v_b", tag="v_b", align_bytes=64)
         nc.vector.tensor_copy(v_b[:].bitcast(F32).rearrange("p (e u) -> p e u", u=2), v_ps[:].rearrange("p u e -> p e u"))
 

@@ -21,6 +21,7 @@ AXIS_X = mybir.AxisListType.X
 P = 128
 N, T, D, DV, NQ, NEW = 512, 1024, 512, 128, 128, 256
 SPLIT = (512, 0, 0, 0)
+PIECES = ((0, 256), (256, 384), (384, 512))
 FLOPS = 2 * NQ * N * (D + DV)
 
 
@@ -83,8 +84,8 @@ def tile_attend_kv_append256_sink_kernel(tc, qT, kT, vT, new_kT, new_vT, vs, sin
             if t < 3:
                 nc.scalar.activation(k_v[:, :, t], kb[t][:].indirect(offs_sb[:]), COPY)
             else:
-                for h in range(2):
-                    nc.scalar.activation(k_v[:, h * H : (h + 1) * H, t], kb[t][:].indirect(offs_sb[:, h * H // 16 : (h + 1) * H // 16]), COPY)
+                for lo, hi in PIECES:
+                    nc.scalar.activation(k_v[:, lo:hi, t], kb[t][:].indirect(offs_sb[:, lo // 16 : hi // 16]), COPY)
 
         nc.vector.tensor_copy(vpool[:].indirect(slots_sb[:]), newv[:])
 
@@ -102,15 +103,16 @@ def tile_attend_kv_append256_sink_kernel(tc, qT, kT, vT, new_kT, new_vT, vs, sin
         k_s = held.tile([P, N], U8, name="k_s", align_bytes=64)
         score = [psum.tile([P, H], F32, name=f"score{h}", tag=f"score{h}") for h in range(2)]
 
-        def scores(h):
-            c = slice(h * H, (h + 1) * H)
-            nc.vector.quantize_mx(out=k_c[:, c].bitcast(FP8X4), scales=k_s[:, c], in_=k_in[:, h * 4 * H : (h + 1) * 4 * H])
-            nc.tensor.matmul_mx(score[h][:], lhsT=q_c[:].bitcast(FP8X4), lhsT_scale=q_s[:], rhs=k_c[:, c].bitcast(FP8X4), rhs_scale=k_s[:, c], start=True, stop=True)
+        def scores(lo, hi):
+            c = slice(lo, hi)
+            nc.vector.quantize_mx(out=k_c[:, c].bitcast(FP8X4), scales=k_s[:, c], in_=k_in[:, 4 * lo : 4 * hi])
+            nc.tensor.matmul_mx(score[lo // H][:, lo % H : lo % H + hi - lo], lhsT=q_c[:].bitcast(FP8X4), lhsT_scale=q_s[:], rhs=k_c[:, c].bitcast(FP8X4), rhs_scale=k_s[:, c], start=True, stop=True)
 
         nc.vector.quantize_mx(out=q_c[:].bitcast(FP8X4), scales=q_s[:], in_=q_b)
-        scores(0)
+        scores(*PIECES[0])
         gather_v(3 * Q, N)
-        scores(1)
+        scores(*PIECES[1])
+        scores(*PIECES[2])
 
 
         negm = held.tile([P, 1], F32, name="negm")

@@ -70,10 +70,11 @@ def tile_attend_kv_append256_sink_kernel(tc, qT, kT, vT, new_kT, new_vT, vs, sin
         H = N // 2
         kb = [held.tile([P, T], BF16, name=f"kb{t}", tag=f"kb{t}", align_bytes=64) for t in range(4)]
         Q = N // 4
-        stage = held.tile([P, 4 * N + 2 * N - 2 * Q], BF16, name="stage", align_bytes=64)
-        k_in = stage[:, : 4 * N]
-        v_q = stage[:, 4 * N - Q : 5 * N - Q]
-        q_b = stage[:, 5 * N - 2 * Q :]
+        k_all = held.tile([P, 4 * N], BF16, name="k_all", align_bytes=64)
+        k_in = k_all[:]
+        stage = held.tile([P, H + N], BF16, name="stage", align_bytes=64)
+        v_q = stage[:, :N]
+        q_b = stage[:, H:]
         k_v = k_in.rearrange("p (n t) -> p n t", t=4)
         for t in range(4):
             split = SPLIT[t]
@@ -92,7 +93,7 @@ def tile_attend_kv_append256_sink_kernel(tc, qT, kT, vT, new_kT, new_vT, vs, sin
         def gather_v(lo, hi):
             nc.vector.tensor_copy(v_q[:, lo:hi], vpool[:].indirect(offs_sb[:, lo // 16 : hi // 16]))
 
-        gather_v(Q, 3 * Q)
+        gather_v(0, H)
         negsink = held.tile([P, 1], F32, name="negsink")
         nc.gpsimd.tensor_scalar(negsink[:], sink_sb[:], -1.0, 0.0, op0=MULT, op1=ADD)
         nc.gpsimd.tensor_scalar(q_b.rearrange("p (q t) -> p q t", t=4), q_raw[:].rearrange("p t q -> p q t"), 1.0, 0.0, op0=MULT, op1=ADD)
@@ -110,7 +111,7 @@ def tile_attend_kv_append256_sink_kernel(tc, qT, kT, vT, new_kT, new_vT, vs, sin
 
         nc.vector.quantize_mx(out=q_c[:].bitcast(FP8X4), scales=q_s[:], in_=q_b)
         scores(*PIECES[0])
-        gather_v(3 * Q, N)
+        gather_v(H, N)
         scores(*PIECES[1])
         scores(*PIECES[2])
 
@@ -119,7 +120,6 @@ def tile_attend_kv_append256_sink_kernel(tc, qT, kT, vT, new_kT, new_vT, vs, sin
         neg_score = held.tile([P, 4, P], F32, name="neg_score")
         negm_0 = held.tile([P, 1], F32, name="negm_0", tag="v_b", align_bytes=64)
         nc.vector.tensor_scalar(neg_score[:, :, : P // 2], score[0][:].rearrange("q (s t) -> q t s", t=4), -1.0, negsink[:], op0=MULT, op1=MIN, accum_out=negm_0[:])
-        gather_v(0, Q)
         nc.vector.tensor_scalar(neg_score[:, :, P // 2 :], score[1][:].rearrange("q (s t) -> q t s", t=4), -1.0, negm_0[:], op0=MULT, op1=MIN, accum_out=negm[:])
 
         v_ps = psum.tile([P, 2, DV], F32, name="v_ps", tag="score0")

@@ -22,6 +22,7 @@ P = 128
 N, T, D, DV, NQ, NEW = 512, 1024, 512, 128, 128, 256
 SPLIT = (512, 0, 0, 0)
 PIECES = ((0, 256), (256, 384), (384, 512))
+V_FIRST = 384
 FLOPS = 2 * NQ * N * (D + DV)
 
 
@@ -72,9 +73,9 @@ def tile_attend_kv_append256_sink_kernel(tc, qT, kT, vT, new_kT, new_vT, vs, sin
         Q = N // 4
         k_all = held.tile([P, 4 * N], BF16, name="k_all", align_bytes=64)
         k_in = k_all[:]
-        stage = held.tile([P, H + N], BF16, name="stage", align_bytes=64)
+        stage = held.tile([P, V_FIRST + N], BF16, name="stage", align_bytes=64)
         v_q = stage[:, :N]
-        q_b = stage[:, H:]
+        q_b = stage[:, V_FIRST:]
         k_v = k_in.rearrange("p (n t) -> p n t", t=4)
         for t in range(4):
             split = SPLIT[t]
@@ -93,7 +94,7 @@ def tile_attend_kv_append256_sink_kernel(tc, qT, kT, vT, new_kT, new_vT, vs, sin
         def gather_v(lo, hi):
             nc.vector.tensor_copy(v_q[:, lo:hi], vpool[:].indirect(offs_sb[:, lo // 16 : hi // 16]))
 
-        gather_v(0, H)
+        gather_v(0, V_FIRST)
         negsink = held.tile([P, 1], F32, name="negsink")
         nc.gpsimd.tensor_scalar(negsink[:], sink_sb[:], -1.0, 0.0, op0=MULT, op1=ADD)
         nc.gpsimd.tensor_scalar(q_b.rearrange("p (q t) -> p q t", t=4), q_raw[:].rearrange("p t q -> p q t"), 1.0, 0.0, op0=MULT, op1=ADD)
@@ -111,7 +112,7 @@ def tile_attend_kv_append256_sink_kernel(tc, qT, kT, vT, new_kT, new_vT, vs, sin
 
         nc.vector.quantize_mx(out=q_c[:].bitcast(FP8X4), scales=q_s[:], in_=q_b)
         scores(*PIECES[0])
-        gather_v(H, N)
+        gather_v(V_FIRST, N)
         scores(*PIECES[1])
         scores(*PIECES[2])
 

@@ -52,9 +52,10 @@ def tile_attend_kv_append256_sink_kernel(tc, qT, kT, vT, new_kT, new_vT, vs, sin
             nc.sync.dma_start(newk[t], newk_v[:, t, :])
             if t == 0:
                 nc.sync.dma_start(slots_sb[:], slots)
+            if t == 1:
+                nc.sync.dma_start(sink_sb[:], sink.rearrange("b q o -> (b q) o"))
         nc.sync.dma_start(newv[:], new_vT)
         nc.sync.dma_start(vpool[:], vT)
-        nc.sync.dma_start(sink_sb[:], sink.rearrange("b q o -> (b q) o"))
         nc.sync.dma_start(q_raw[:], qT.rearrange("b (p t) q -> p (b t) q", t=4))
 
         ident_f = held.tile([P, P], F32, name="ident_f")
@@ -67,6 +68,9 @@ def tile_attend_kv_append256_sink_kernel(tc, qT, kT, vT, new_kT, new_vT, vs, sin
             nc.tensor.transpose(vs_ps[:, t, :], vs_g[:, t::4], ident_f[:])
         vs_col = held.tile([P, 4], F32, name="vs_col")
         nc.scalar.copy(vs_col[:], vs_ps[:, :, P - 1])
+
+        negsink = held.tile([P, 1], F32, name="negsink")
+        nc.gpsimd.tensor_scalar(negsink[:], sink_sb[:], -1.0, 0.0, op0=MULT, op1=ADD)
 
         H = N // 2
         kb = [held.tile([P, T], BF16, name=f"kb{t}", tag=f"kb{t}", align_bytes=64) for t in range(4)]
@@ -95,8 +99,6 @@ def tile_attend_kv_append256_sink_kernel(tc, qT, kT, vT, new_kT, new_vT, vs, sin
             nc.vector.tensor_copy(v_q[:, lo:hi], vpool[:].indirect(offs_sb[:, lo // 16 : hi // 16]))
 
         gather_v(0, V_FIRST)
-        negsink = held.tile([P, 1], F32, name="negsink")
-        nc.gpsimd.tensor_scalar(negsink[:], sink_sb[:], -1.0, 0.0, op0=MULT, op1=ADD)
         nc.gpsimd.tensor_scalar(q_b.rearrange("p (q t) -> p q t", t=4), q_raw[:].rearrange("p t q -> p q t"), 1.0, 0.0, op0=MULT, op1=ADD)
 
         q_c = held.tile([P, NQ], U32, name="q_c", align_bytes=64)

@@ -45,6 +45,7 @@ def tile_attend_kv_append256_sink_kernel(tc, qT, kT, vT, new_kT, new_vT, vs, sin
         kT_v = kT.rearrange("(p t) n -> p t n", t=4)
         newk_v = new_kT.rearrange("(p t) n -> p t n", t=4)
         nc.scalar.dma_start(vs_sb[P - 1 : P, :], vs[0:1, :])
+        nc.scalar.dma_start(sink_sb[:], sink.rearrange("b q o -> (b q) o"))
         nc.vector.memset(vs_sb[: P - 1, :], 0.0)
         nc.sync.dma_start(offs_sb[:], offs)
         for t in range(4):
@@ -52,8 +53,6 @@ def tile_attend_kv_append256_sink_kernel(tc, qT, kT, vT, new_kT, new_vT, vs, sin
             nc.sync.dma_start(newk[t], newk_v[:, t, :])
             if t == 0:
                 nc.sync.dma_start(slots_sb[:], slots)
-            if t == 1:
-                nc.sync.dma_start(sink_sb[:], sink.rearrange("b q o -> (b q) o"))
         nc.sync.dma_start(newv[:], new_vT)
         nc.sync.dma_start(vpool[:], vT)
         nc.sync.dma_start(q_raw[:], qT.rearrange("b (p t) q -> p (b t) q", t=4))

@@ -40,12 +40,13 @@ def tile_attend_kv_append256_sink_kernel(tc, qT, kT, vT, new_kT, new_vT, vs, sin
         kpool = [held.tile([P, T], F32, name=f"kpool{t}", tag=f"kpool{t}", align_bytes=64) for t in range(4)]
         q_raw = held.tile([P, 4, NQ], F32, name="q_raw", tag="q_raw", align_bytes=64)
         vs_sb = held.tile([P, T], F32, name="vs_sb")
-        sink_sb = held.tile([P, 1], F32, name="sink_sb", tag="ring", align_bytes=64)
+        sink_row = held.tile([P, NQ], F32, name="sink_row")
 
         kT_v = kT.rearrange("(p t) n -> p t n", t=4)
         newk_v = new_kT.rearrange("(p t) n -> p t n", t=4)
         nc.scalar.dma_start(vs_sb[P - 1 : P, :], vs[0:1, :])
-        nc.scalar.dma_start(sink_sb[:], sink.rearrange("b q o -> (b q) o"))
+        nc.scalar.dma_start(sink_row[P - 1 : P, :], sink.rearrange("b q o -> (b o) q"))
+        nc.gpsimd.memset(sink_row[: P - 1, :], 0.0)
         nc.vector.memset(vs_sb[: P - 1, :], 0.0)
         nc.sync.dma_start(offs_sb[:], offs)
         for t in range(4):
@@ -69,7 +70,9 @@ def tile_attend_kv_append256_sink_kernel(tc, qT, kT, vT, new_kT, new_vT, vs, sin
         nc.scalar.copy(vs_col[:], vs_ps[:, :, P - 1])
 
         negsink = held.tile([P, 1], F32, name="negsink")
-        nc.gpsimd.tensor_scalar(negsink[:], sink_sb[:], -1.0, 0.0, op0=MULT, op1=ADD)
+        sink_ps = psum.tile([P, P], F32, name="sink_ps")
+        nc.tensor.transpose(sink_ps[:], sink_row[:], ident_f[:])
+        nc.scalar.activation(negsink[:], sink_ps[:, P - 1 :], COPY, scale=-1.0)
 
         H = N // 2
         kb = [held.tile([P, T], BF16, name=f"kb{t}", tag=f"kb{t}", align_bytes=64) for t in range(4)]

@@ -48,12 +48,13 @@ def tile_attend_kv_append256_sink_kernel(tc, qT, kT, vT, new_kT, new_vT, vs, sin
         nc.scalar.dma_start(sink_row[P - 1 : P, :], sink.rearrange("b q o -> (b o) q"))
         nc.gpsimd.memset(sink_row[: P - 1, :], 0.0)
         nc.vector.memset(vs_sb[: P - 1, :], 0.0)
+        nc.sync.dma_start(newk[0], newk_v[:, 0, :])
         nc.sync.dma_start(offs_sb[:], offs)
+        nc.sync.dma_start(slots_sb[:], slots)
         for t in range(4):
             nc.sync.dma_start(kpool[t][:], kT_v[:, t, :])
-            nc.sync.dma_start(newk[t], newk_v[:, t, :])
-            if t == 0:
-                nc.sync.dma_start(slots_sb[:], slots)
+            if t > 0:
+                nc.sync.dma_start(newk[t], newk_v[:, t, :])
         nc.sync.dma_start(newv[:], new_vT)
         nc.sync.dma_start(vpool[:], vT)
         nc.sync.dma_start(q_raw[:], qT.rearrange("b (p t) q -> p (b t) q", t=4))

@@ -89,7 +89,7 @@ def tile_attend_kv_append256_sink_kernel(tc, qT, kT, vT, new_kT, new_vT, vs, sin
             nc.vector.tensor_copy(kpool[t][:].indirect(slots_sb[:]), newk[t])
             if split:
                 nc.scalar.copy(kb[t][:, :split], kpool[t][:, :split])
-            nc.gpsimd.tensor_scalar(kb[t][:, split:], kpool[t][:, split:], 1.0, 0.0, op0=MULT, op1=ADD)
+            nc.gpsimd.tensor_copy(kb[t][:, split:], kpool[t][:, split:])
             if t < 3:
                 nc.scalar.activation(k_v[:, :, t], kb[t][:].indirect(offs_sb[:]), COPY)
             else:

@@ -6,13 +6,11 @@ from concourse.masks import make_identity
 F32 = mybir.dt.float32
 BF16 = mybir.dt.bfloat16
 U32 = mybir.dt.uint32
-I32 = mybir.dt.int32
 U16 = mybir.dt.uint16
 U8 = mybir.dt.uint8
 FP8X4 = mybir.dt.float8_e4m3fn_x4
 MULT = mybir.AluOpType.mult
 ADD = mybir.AluOpType.add
-MAX = mybir.AluOpType.max
 MIN = mybir.AluOpType.min
 EXP = mybir.ActivationFunctionType.Exp
 COPY = mybir.ActivationFunctionType.Copy
@@ -20,9 +18,7 @@ AXIS_X = mybir.AxisListType.X
 
 P = 128
 N, T, D, DV, NQ, NEW = 512, 1024, 512, 128, 128, 256
-SPLIT = (512, 0, 0, 0)
-PIECES = ((0, 256), (256, 384), (384, 512))
-V_FIRST = 384
+HALF = N // 2
 FLOPS = 2 * NQ * N * (D + DV)
 
 
@@ -36,9 +32,9 @@ def tile_attend_kv_append256_sink_kernel(tc, qT, kT, vT, new_kT, new_vT, vs, sin
         offs_sb = held.tile([P, N // 16], U16, name="offs_sb")
         newv = held.tile([P, NEW], F32, name="newv")
         vpool = held.tile([P, T], F32, name="vpool")
-        newk = [held.tile([P, NEW], F32, name=f"newk{t}")[:] for t in range(4)]
-        kpool = [held.tile([P, T], F32, name=f"kpool{t}", tag=f"kpool{t}", align_bytes=64) for t in range(4)]
-        q_raw = held.tile([P, 4, NQ], F32, name="q_raw", tag="q_raw", align_bytes=64)
+        newk = [held.tile([P, NEW], F32, name=f"newk{t}") for t in range(4)]
+        kpool = [held.tile([P, T], F32, name=f"kpool{t}") for t in range(4)]
+        q_raw = held.tile([P, 4, NQ], F32, name="q_raw")
         vs_sb = held.tile([P, T], F32, name="vs_sb")
         sink_row = held.tile([P, NQ], F32, name="sink_row")
 
@@ -46,81 +42,79 @@ def tile_attend_kv_append256_sink_kernel(tc, qT, kT, vT, new_kT, new_vT, vs, sin
         newk_v = new_kT.rearrange("(p t) n -> p t n", t=4)
         nc.scalar.dma_start(vs_sb[P - 1 : P, :], vs[0:1, :])
         nc.scalar.dma_start(sink_row[P - 1 : P, :], sink.rearrange("b q o -> (b o) q"))
-        nc.gpsimd.memset(sink_row[: P - 1, :], 0.0)
         nc.vector.memset(vs_sb[: P - 1, :], 0.0)
-        nc.sync.dma_start(newk[0], newk_v[:, 0, :])
+        nc.scalar.activation(sink_row[: P - 1, :], vs_sb[: P - 1, :NQ], COPY)
+        nc.sync.dma_start(newk[0][:], newk_v[:, 0, :])
         nc.sync.dma_start(offs_sb[:], offs)
         nc.sync.dma_start(slots_sb[:], slots)
         for t in range(4):
             nc.sync.dma_start(kpool[t][:], kT_v[:, t, :])
             if t > 0:
-                nc.sync.dma_start(newk[t], newk_v[:, t, :])
+                nc.sync.dma_start(newk[t][:], newk_v[:, t, :])
+        nc.sync.dma_start(q_raw[:], qT.rearrange("b (p t) q -> p (b t) q", t=4))
         nc.sync.dma_start(newv[:], new_vT)
         nc.sync.dma_start(vpool[:], vT)
-        nc.sync.dma_start(q_raw[:], qT.rearrange("b (p t) q -> p (b t) q", t=4))
 
-        ident_f = held.tile([P, P], F32, name="ident_f")
-        make_identity(nc, ident_f[:])
+        ident = held.tile([P, P], F32, name="ident")
+        make_identity(nc, ident[:])
 
-        vs_g = held.tile([P, N], F32, name="vs_g", align_bytes=64)
-        nc.vector.tensor_copy(vs_g[:], vs_sb[:].indirect(offs_sb[:]))
-        vs_ps = psum.tile([P, 4, P], F32, name="vs_ps")
-        for t in range(4):
-            nc.tensor.transpose(vs_ps[:, t, :], vs_g[:, t::4], ident_f[:])
-        vs_col = held.tile([P, 4], F32, name="vs_col")
-        nc.scalar.copy(vs_col[:], vs_ps[:, :, P - 1])
+        def scatter(engine, pool_tile, new_tile):
+            if engine == "vector":
+                nc.vector.tensor_copy(pool_tile[:].indirect(slots_sb[:]), new_tile[:])
+            else:
+                nc.scalar.activation(pool_tile[:].indirect(slots_sb[:]), new_tile[:], COPY)
+
+        def gather(engine, dst, pool_tile, lo, hi):
+            window = pool_tile[:].indirect(offs_sb[:, lo // 16 : hi // 16])
+            if engine == "vector":
+                nc.vector.tensor_copy(dst, window)
+            else:
+                nc.scalar.activation(dst, window, COPY)
 
         negsink = held.tile([P, 1], F32, name="negsink")
         sink_ps = psum.tile([P, P], F32, name="sink_ps")
-        nc.tensor.transpose(sink_ps[:], sink_row[:], ident_f[:])
+        nc.tensor.transpose(sink_ps[:], sink_row[:], ident[:])
         nc.scalar.activation(negsink[:], sink_ps[:, P - 1 :], COPY, scale=-1.0)
 
-        H = N // 2
-        kb = [held.tile([P, T], BF16, name=f"kb{t}", tag=f"kb{t}", align_bytes=64) for t in range(4)]
-        Q = N // 4
-        k_all = held.tile([P, 4 * N], BF16, name="k_all", align_bytes=64)
-        k_in = k_all[:]
-        stage = held.tile([P, V_FIRST + N], BF16, name="stage", align_bytes=64)
-        v_q = stage[:, :N]
-        q_b = stage[:, V_FIRST:]
-        k_v = k_in.rearrange("p (n t) -> p n t", t=4)
+        vs_g = held.tile([P, N], F32, name="vs_g")
+        gather("vector", vs_g[:], vs_sb, 0, N)
+        vs_ps = psum.tile([P, 4, P], F32, name="vs_ps")
         for t in range(4):
-            split = SPLIT[t]
-            nc.vector.tensor_copy(kpool[t][:].indirect(slots_sb[:]), newk[t])
-            if split:
-                nc.scalar.copy(kb[t][:, :split], kpool[t][:, :split])
-            nc.gpsimd.tensor_copy(kb[t][:, split:], kpool[t][:, split:])
+            nc.tensor.transpose(vs_ps[:, t, :], vs_g[:, t::4], ident[:])
+        vs_col = held.tile([P, 4], F32, name="vs_col")
+        nc.scalar.activation(vs_col[:], vs_ps[:, :, P - 1], COPY)
+
+        k_g = held.tile([P, 4 * N], BF16, name="k_g", align_bytes=64)
+        for t in range(4):
+            engine = ("vector", "scalar")[t % 2]
+            scatter(engine, kpool[t], newk[t])
             if t < 3:
-                nc.scalar.activation(k_v[:, :, t], kb[t][:].indirect(offs_sb[:]), COPY)
+                gather(engine, k_g[:, t * N : (t + 1) * N], kpool[t], 0, N)
             else:
-                for lo, hi in PIECES:
-                    nc.scalar.activation(k_v[:, lo:hi, t], kb[t][:].indirect(offs_sb[:, lo // 16 : hi // 16]), COPY)
+                gather("vector", k_g[:, t * N : t * N + HALF], kpool[t], 0, HALF)
+                gather("scalar", k_g[:, t * N + HALF : (t + 1) * N], kpool[t], HALF, N)
 
-        nc.vector.tensor_copy(vpool[:].indirect(slots_sb[:]), newv[:])
-
-        def gather_v(lo, hi):
-            nc.vector.tensor_copy(v_q[:, lo:hi], vpool[:].indirect(offs_sb[:, lo // 16 : hi // 16]))
-
-        gather_v(0, V_FIRST)
-        nc.gpsimd.tensor_scalar(q_b.rearrange("p (q t) -> p q t", t=4), q_raw[:].rearrange("p t q -> p q t"), 1.0, 0.0, op0=MULT, op1=ADD)
-
+        q_b = held.tile([P, NQ * 4], BF16, name="q_b", align_bytes=64)
+        nc.gpsimd.tensor_copy(q_b[:].rearrange("p (q t) -> p q t", t=4), q_raw[:].rearrange("p t q -> p q t"))
         q_c = held.tile([P, NQ], U32, name="q_c", align_bytes=64)
         q_s = held.tile([P, NQ], U8, name="q_s", align_bytes=64)
-        k_c = held.tile([P, N], U32, name="k_c", tag="q_raw", align_bytes=64)
+        nc.vector.quantize_mx(out=q_c[:].bitcast(FP8X4), scales=q_s[:], in_=q_b[:])
+
+        v_q = held.tile([P, N], BF16, name="v_q", align_bytes=64)
+        scatter("scalar", vpool, newv)
+        gather("scalar", v_q[:], vpool, 0, N)
+
+        k_in = [held.tile([P, HALF * 4], BF16, name=f"k_in{h}", align_bytes=64) for h in range(2)]
+        k_c = held.tile([P, N], U32, name="k_c", align_bytes=64)
         k_s = held.tile([P, N], U8, name="k_s", align_bytes=64)
-        score = [psum.tile([P, H], F32, name=f"score{h}", tag=f"score{h}") for h in range(2)]
-
-        def scores(lo, hi):
-            c = slice(lo, hi)
-            nc.vector.quantize_mx(out=k_c[:, c].bitcast(FP8X4), scales=k_s[:, c], in_=k_in[:, 4 * lo : 4 * hi])
-            nc.tensor.matmul_mx(score[lo // H][:, lo % H : lo % H + hi - lo], lhsT=q_c[:].bitcast(FP8X4), lhsT_scale=q_s[:], rhs=k_c[:, c].bitcast(FP8X4), rhs_scale=k_s[:, c], start=True, stop=True)
-
-        nc.vector.quantize_mx(out=q_c[:].bitcast(FP8X4), scales=q_s[:], in_=q_b)
-        scores(*PIECES[0])
-        gather_v(V_FIRST, N)
-        scores(*PIECES[1])
-        scores(*PIECES[2])
-
+        score = [psum.tile([P, HALF], F32, name=f"score{h}", tag=f"score{h}") for h in range(2)]
+        planes = k_g[:].rearrange("p (t n) -> p n t", t=4)
+        for h in range(2):
+            nc.vector.tensor_copy(k_in[h][:].rearrange("p (n t) -> p n t", t=4), planes[:, h * HALF : (h + 1) * HALF, :])
+        for h in range(2):
+            c = slice(h * HALF, (h + 1) * HALF)
+            nc.vector.quantize_mx(out=k_c[:, c].bitcast(FP8X4), scales=k_s[:, c], in_=k_in[h][:])
+            nc.tensor.matmul_mx(score[h][:], lhsT=q_c[:].bitcast(FP8X4), lhsT_scale=q_s[:], rhs=k_c[:, c].bitcast(FP8X4), rhs_scale=k_s[:, c], start=True, stop=True)
 
         negm = held.tile([P, 1], F32, name="negm")
         neg_score = held.tile([P, 4, P], F32, name="neg_score")
@@ -130,7 +124,7 @@ def tile_attend_kv_append256_sink_kernel(tc, qT, kT, vT, new_kT, new_vT, vs, sin
 
         v_ps = psum.tile([P, 2, DV], F32, name="v_ps", tag="score0")
         for u in range(2):
-            nc.tensor.transpose(v_ps[:, u, :], v_q.bitcast(F32)[:, u::2], ident_f[:])
+            nc.tensor.transpose(v_ps[:, u, :], v_q[:].bitcast(F32)[:, u::2], ident[:])
         v_b = held.tile([P, DV * 4], BF16, name="v_b", tag="v_b", align_bytes=64)
         nc.vector.tensor_copy(v_b[:].bitcast(F32).rearrange("p (e u) -> p e u", u=2), v_ps[:].rearrange("p u e -> p e u"))
 
@@ -149,7 +143,7 @@ def tile_attend_kv_append256_sink_kernel(tc, qT, kT, vT, new_kT, new_vT, vs, sin
         for h in range(2):
             p_ps = psum.tile([P, 2, NQ], F32, name=f"p_ps{h}")
             for t in range(2):
-                nc.tensor.transpose(p_ps[:, t, :], p_sb[:, 2 * h + t, :], ident_f[:])
+                nc.tensor.transpose(p_ps[:, t, :], p_sb[:, 2 * h + t, :], ident[:])
             for c in ((slice(0, NQ),), (slice(0, NQ // 2), slice(NQ // 2, NQ)))[h]:
                 nc.vector.tensor_tensor(
                     w_b[:, c, 2 * h : 2 * h + 2],

@@ -6,6 +6,7 @@ from concourse.masks import make_identity
 F32 = mybir.dt.float32
 BF16 = mybir.dt.bfloat16
 U32 = mybir.dt.uint32
+I32 = mybir.dt.int32
 U16 = mybir.dt.uint16
 U8 = mybir.dt.uint8
 FP8X4 = mybir.dt.float8_e4m3fn_x4
@@ -48,10 +49,11 @@ def tile_attend_kv_append256_sink_kernel(tc, qT, kT, vT, new_kT, new_vT, vs, sin
         nc.sync.dma_start(offs_sb[:], offs)
         nc.sync.dma_start(slots_sb[:], slots)
         for t in range(4):
+            if t == 3:
+                nc.sync.dma_start(q_raw[:], qT.rearrange("b (p t) q -> p (b t) q", t=4))
             nc.sync.dma_start(kpool[t][:], kT_v[:, t, :])
             if t > 0:
                 nc.sync.dma_start(newk[t][:], newk_v[:, t, :])
-        nc.sync.dma_start(q_raw[:], qT.rearrange("b (p t) q -> p (b t) q", t=4))
         nc.sync.dma_start(newv[:], new_vT)
         nc.sync.dma_start(vpool[:], vT)
 
@@ -84,15 +86,11 @@ def tile_attend_kv_append256_sink_kernel(tc, qT, kT, vT, new_kT, new_vT, vs, sin
         vs_col = held.tile([P, 4], F32, name="vs_col")
         nc.scalar.activation(vs_col[:], vs_ps[:, :, P - 1], COPY)
 
-        k_g = held.tile([P, 4 * N], BF16, name="k_g", align_bytes=64)
+        pairs = [held.tile([P, 2, HALF, 2], BF16, name=f"pairs{h}", align_bytes=64) for h in range(2)]
         for t in range(4):
-            engine = ("vector", "scalar")[t % 2]
-            scatter(engine, kpool[t], newk[t])
-            if t < 3:
-                gather(engine, k_g[:, t * N : (t + 1) * N], kpool[t], 0, N)
-            else:
-                gather("vector", k_g[:, t * N : t * N + HALF], kpool[t], 0, HALF)
-                gather("scalar", k_g[:, t * N + HALF : (t + 1) * N], kpool[t], HALF, N)
+            scatter("vector" if t == 0 else "scalar", kpool[t], newk[t])
+            for h in range(2):
+                gather("vector", pairs[h][:, t // 2, :, t % 2], kpool[t], h * HALF, (h + 1) * HALF)
 
         q_b = held.tile([P, NQ * 4], BF16, name="q_b", align_bytes=64)
         nc.gpsimd.tensor_copy(q_b[:].rearrange("p (q t) -> p q t", t=4), q_raw[:].rearrange("p t q -> p q t"))
@@ -108,9 +106,9 @@ def tile_attend_kv_append256_sink_kernel(tc, qT, kT, vT, new_kT, new_vT, vs, sin
         k_c = held.tile([P, N], U32, name="k_c", align_bytes=64)
         k_s = held.tile([P, N], U8, name="k_s", align_bytes=64)
         score = [psum.tile([P, HALF], F32, name=f"score{h}", tag=f"score{h}") for h in range(2)]
-        planes = k_g[:].rearrange("p (t n) -> p n t", t=4)
         for h in range(2):
-            nc.vector.tensor_copy(k_in[h][:].rearrange("p (n t) -> p n t", t=4), planes[:, h * HALF : (h + 1) * HALF, :])
+            words = pairs[h][:].rearrange("p u n e -> p (u n e)").bitcast(I32).rearrange("p (u n) -> p n u", u=2)
+            nc.vector.tensor_copy(k_in[h][:].bitcast(I32).rearrange("p (n u) -> p n u", u=2), words)
         for h in range(2):
             c = slice(h * HALF, (h + 1) * HALF)
             nc.vector.quantize_mx(out=k_c[:, c].bitcast(FP8X4), scales=k_s[:, c], in_=k_in[h][:])

@@ -33,8 +33,8 @@ def tile_attend_kv_append256_sink_kernel(tc, qT, kT, vT, new_kT, new_vT, vs, sin
         offs_sb = held.tile([P, N // 16], U16, name="offs_sb")
         newv = held.tile([P, NEW], F32, name="newv")
         vpool = held.tile([P, T], F32, name="vpool")
-        newk = [held.tile([P, NEW], F32, name=f"newk{t}") for t in range(4)]
-        kpool = [held.tile([P, T], F32, name=f"kpool{t}") for t in range(4)]
+        newk = [held.tile([P, NEW], F32, name=f"newk{t}", tag=f"newk{t}") for t in range(4)]
+        kpool = [held.tile([P, T], F32, name=f"kpool{t}", tag=f"kpool{t}", align_bytes=64) for t in range(4)]
         q_raw = held.tile([P, 4, NQ], F32, name="q_raw")
         vs_sb = held.tile([P, T], F32, name="vs_sb")
         sink_row = held.tile([P, NQ], F32, name="sink_row")
@@ -49,11 +49,10 @@ def tile_attend_kv_append256_sink_kernel(tc, qT, kT, vT, new_kT, new_vT, vs, sin
         nc.sync.dma_start(offs_sb[:], offs)
         nc.sync.dma_start(slots_sb[:], slots)
         for t in range(4):
-            if t == 3:
-                nc.sync.dma_start(q_raw[:], qT.rearrange("b (p t) q -> p (b t) q", t=4))
             nc.sync.dma_start(kpool[t][:], kT_v[:, t, :])
             if t > 0:
                 nc.sync.dma_start(newk[t][:], newk_v[:, t, :])
+        nc.sync.dma_start(q_raw[:], qT.rearrange("b (p t) q -> p (b t) q", t=4))
         nc.sync.dma_start(newv[:], new_vT)
         nc.sync.dma_start(vpool[:], vT)
 
@@ -79,24 +78,26 @@ def tile_attend_kv_append256_sink_kernel(tc, qT, kT, vT, new_kT, new_vT, vs, sin
         nc.scalar.activation(negsink[:], sink_ps[:, P - 1 :], COPY, scale=-1.0)
 
         vs_g = held.tile([P, N], F32, name="vs_g")
-        gather("vector", vs_g[:], vs_sb, 0, N)
+        gather("scalar", vs_g[:], vs_sb, 0, N)
         vs_ps = psum.tile([P, 4, P], F32, name="vs_ps")
         for t in range(4):
             nc.tensor.transpose(vs_ps[:, t, :], vs_g[:, t::4], ident[:])
-        vs_col = held.tile([P, 4], F32, name="vs_col")
-        nc.scalar.activation(vs_col[:], vs_ps[:, :, P - 1], COPY)
 
         pairs = [held.tile([P, 2, HALF, 2], BF16, name=f"pairs{h}", align_bytes=64) for h in range(2)]
         for t in range(4):
             scatter("vector" if t == 0 else "scalar", kpool[t], newk[t])
+            if t == 0:
+                vs_col = held.tile([P, 4], F32, name="vs_col", tag="newk0")
+                nc.vector.tensor_copy(vs_col[:], vs_ps[:, :, P - 1])
             for h in range(2):
                 gather("vector", pairs[h][:, t // 2, :, t % 2], kpool[t], h * HALF, (h + 1) * HALF)
+            if t == 2:
+                q_b = held.tile([P, NQ * 4], BF16, name="q_b", align_bytes=64)
+                nc.gpsimd.tensor_copy(q_b[:].rearrange("p (q t) -> p q t", t=4), q_raw[:].rearrange("p t q -> p q t"))
+                q_c = held.tile([P, NQ], U32, name="q_c", align_bytes=64)
+                q_s = held.tile([P, NQ], U8, name="q_s", align_bytes=64)
+                nc.vector.quantize_mx(out=q_c[:].bitcast(FP8X4), scales=q_s[:], in_=q_b[:])
 
-        q_b = held.tile([P, NQ * 4], BF16, name="q_b", align_bytes=64)
-        nc.gpsimd.tensor_copy(q_b[:].rearrange("p (q t) -> p q t", t=4), q_raw[:].rearrange("p t q -> p q t"))
-        q_c = held.tile([P, NQ], U32, name="q_c", align_bytes=64)
-        q_s = held.tile([P, NQ], U8, name="q_s", align_bytes=64)
-        nc.vector.quantize_mx(out=q_c[:].bitcast(FP8X4), scales=q_s[:], in_=q_b[:])
 
         v_q = held.tile([P, N], BF16, name="v_q", align_bytes=64)
         scatter("scalar", vpool, newv)

@@ -27,6 +27,7 @@ def tile_attend_kv_append256_sink_kernel(tc, qT, kT, vT, new_kT, new_vT, vs, sin
     nc = tc.nc
     with ExitStack() as ctx:
         held = ctx.enter_context(tc.tile_pool(name="held", bufs=1))
+        shared = ctx.enter_context(tc.tile_pool(name="shared", bufs=1))
         psum = ctx.enter_context(tc.psum_pool(name="psum", bufs=1))
 
         slots_sb = held.tile([P, NEW // 16], U16, name="slots_sb")
@@ -35,7 +36,7 @@ def tile_attend_kv_append256_sink_kernel(tc, qT, kT, vT, new_kT, new_vT, vs, sin
         vpool = held.tile([P, T], F32, name="vpool")
         newk = [held.tile([P, NEW], F32, name=f"newk{t}", tag=f"newk{t}") for t in range(4)]
         kpool = [held.tile([P, T], F32, name=f"kpool{t}", tag=f"kpool{t}", align_bytes=64) for t in range(4)]
-        q_raw = held.tile([P, 4, NQ], F32, name="q_raw")
+        q_raw = shared.tile([P, 4, NQ], F32, name="q_raw", offset=4 * N - 64)
         vs_sb = held.tile([P, T], F32, name="vs_sb")
         sink_row = held.tile([P, NQ], F32, name="sink_row")
 
@@ -91,29 +92,40 @@ def tile_attend_kv_append256_sink_kernel(tc, qT, kT, vT, new_kT, new_vT, vs, sin
                 nc.vector.tensor_copy(vs_col[:], vs_ps[:, :, P - 1])
             for h in range(2):
                 gather("vector", pairs[h][:, t // 2, :, t % 2], kpool[t], h * HALF, (h + 1) * HALF)
-            if t == 2:
-                q_b = held.tile([P, NQ * 4], BF16, name="q_b", align_bytes=64)
-                nc.gpsimd.tensor_copy(q_b[:].rearrange("p (q t) -> p q t", t=4), q_raw[:].rearrange("p t q -> p q t"))
-                q_c = held.tile([P, NQ], U32, name="q_c", align_bytes=64)
-                q_s = held.tile([P, NQ], U8, name="q_s", align_bytes=64)
-                nc.vector.quantize_mx(out=q_c[:].bitcast(FP8X4), scales=q_s[:], in_=q_b[:])
+
+        q_b = held.tile([P, NQ * 4], BF16, name="q_b", align_bytes=64)
+        nc.scalar.copy(q_b[:].rearrange("p (q t) -> p q t", t=4), q_raw[:].rearrange("p t q -> p q t"))
+        q_c = held.tile([P, NQ], U32, name="q_c", align_bytes=64)
+        q_s = held.tile([P, NQ], U8, name="q_s", align_bytes=64)
+        nc.vector.quantize_mx(out=q_c[:].bitcast(FP8X4), scales=q_s[:], in_=q_b[:])
 
 
         v_q = held.tile([P, N], BF16, name="v_q", align_bytes=64)
         scatter("scalar", vpool, newv)
         gather("scalar", v_q[:], vpool, 0, N)
 
-        k_in = [held.tile([P, HALF * 4], BF16, name=f"k_in{h}", align_bytes=64) for h in range(2)]
-        k_c = held.tile([P, N], U32, name="k_c", align_bytes=64)
+        k_c = shared.tile([P, N], U32, name="k_c", align_bytes=64, offset=0)
         k_s = held.tile([P, N], U8, name="k_s", align_bytes=64)
         score = [psum.tile([P, HALF], F32, name=f"score{h}", tag=f"score{h}") for h in range(2)]
-        for h in range(2):
-            words = pairs[h][:].rearrange("p u n e -> p (u n e)").bitcast(I32).rearrange("p (u n) -> p n u", u=2)
-            nc.vector.tensor_copy(k_in[h][:].bitcast(I32).rearrange("p (n u) -> p n u", u=2), words)
-        for h in range(2):
-            c = slice(h * HALF, (h + 1) * HALF)
-            nc.vector.quantize_mx(out=k_c[:, c].bitcast(FP8X4), scales=k_s[:, c], in_=k_in[h][:])
-            nc.tensor.matmul_mx(score[h][:], lhsT=q_c[:].bitcast(FP8X4), lhsT_scale=q_s[:], rhs=k_c[:, c].bitcast(FP8X4), rhs_scale=k_s[:, c], start=True, stop=True)
+
+        def weave(k_in, lo, hi):
+            words = pairs[lo // HALF][:].rearrange("p u n e -> p (u n e)").bitcast(I32).rearrange("p (u n) -> p n u", u=2)
+            nc.vector.tensor_copy(k_in[:].bitcast(I32).rearrange("p (n u) -> p n u", u=2), words[:, lo % HALF : lo % HALF + hi - lo, :])
+
+        def scores(k_in, lo, hi):
+            c = slice(lo, hi)
+            nc.vector.quantize_mx(out=k_c[:, c].bitcast(FP8X4), scales=k_s[:, c], in_=k_in[:])
+            nc.tensor.matmul_mx(score[lo // HALF][:, lo % HALF : lo % HALF + hi - lo], lhsT=q_c[:].bitcast(FP8X4), lhsT_scale=q_s[:], rhs=k_c[:, c].bitcast(FP8X4), rhs_scale=k_s[:, c], start=True, stop=True)
+
+        first = held.tile([P, 4 * HALF], BF16, name="first", align_bytes=64)
+        third = shared.tile([P, 2 * HALF], BF16, name="third", align_bytes=64, offset=4 * N)
+        fourth = shared.tile([P, 2 * HALF], BF16, name="fourth", align_bytes=64, offset=4 * N + 4 * HALF)
+        weave(first, 0, 256)
+        scores(first, 0, 256)
+        weave(third, 256, 384)
+        weave(fourth, 384, 512)
+        scores(third, 256, 384)
+        scores(fourth, 384, 512)
 
         negm = held.tile([P, 1], F32, name="negm")
         neg_score = held.tile([P, 4, P], F32, name="neg_score")

@@ -84,17 +84,18 @@ def tile_attend_kv_append256_sink_kernel(tc, qT, kT, vT, new_kT, new_vT, vs, sin
         for t in range(4):
             nc.tensor.transpose(vs_ps[:, t, :], vs_g[:, t::4], ident[:])
 
-        pairs = [held.tile([P, 2, HALF, 2], BF16, name=f"pairs{h}", align_bytes=64) for h in range(2)]
+        first = held.tile([P, 4 * HALF], BF16, name="first", align_bytes=64)
+        pairs = held.tile([P, 2, HALF, 2], BF16, name="pairs", align_bytes=64)
         for t in range(4):
             scatter("vector" if t == 0 else "scalar", kpool[t], newk[t])
             if t == 0:
                 vs_col = held.tile([P, 4], F32, name="vs_col", tag="newk0")
                 nc.vector.tensor_copy(vs_col[:], vs_ps[:, :, P - 1])
-            for h in range(2):
-                gather("vector", pairs[h][:, t // 2, :, t % 2], kpool[t], h * HALF, (h + 1) * HALF)
+            gather("vector", first[:, t::4], kpool[t], 0, HALF)
+            gather("vector", pairs[:, t // 2, :, t % 2], kpool[t], HALF, N)
 
         q_b = held.tile([P, NQ * 4], BF16, name="q_b", align_bytes=64)
-        nc.scalar.copy(q_b[:].rearrange("p (q t) -> p q t", t=4), q_raw[:].rearrange("p t q -> p q t"))
+        nc.gpsimd.tensor_copy(q_b[:].rearrange("p (q t) -> p q t", t=4), q_raw[:].rearrange("p t q -> p q t"))
         q_c = held.tile([P, NQ], U32, name="q_c", align_bytes=64)
         q_s = held.tile([P, NQ], U8, name="q_s", align_bytes=64)
         nc.vector.quantize_mx(out=q_c[:].bitcast(FP8X4), scales=q_s[:], in_=q_b[:])
@@ -109,7 +110,7 @@ def tile_attend_kv_append256_sink_kernel(tc, qT, kT, vT, new_kT, new_vT, vs, sin
         score = [psum.tile([P, HALF], F32, name=f"score{h}", tag=f"score{h}") for h in range(2)]
 
         def weave(k_in, lo, hi):
-            words = pairs[lo // HALF][:].rearrange("p u n e -> p (u n e)").bitcast(I32).rearrange("p (u n) -> p n u", u=2)
+            words = pairs[:].rearrange("p u n e -> p (u n e)").bitcast(I32).rearrange("p (u n) -> p n u", u=2)
             nc.vector.tensor_copy(k_in[:].bitcast(I32).rearrange("p (n u) -> p n u", u=2), words[:, lo % HALF : lo % HALF + hi - lo, :])
 
         def scores(k_in, lo, hi):
@@ -117,10 +118,8 @@ def tile_attend_kv_append256_sink_kernel(tc, qT, kT, vT, new_kT, new_vT, vs, sin
             nc.vector.quantize_mx(out=k_c[:, c].bitcast(FP8X4), scales=k_s[:, c], in_=k_in[:])
             nc.tensor.matmul_mx(score[lo // HALF][:, lo % HALF : lo % HALF + hi - lo], lhsT=q_c[:].bitcast(FP8X4), lhsT_scale=q_s[:], rhs=k_c[:, c].bitcast(FP8X4), rhs_scale=k_s[:, c], start=True, stop=True)
 
-        first = held.tile([P, 4 * HALF], BF16, name="first", align_bytes=64)
         third = shared.tile([P, 2 * HALF], BF16, name="third", align_bytes=64, offset=4 * N)
         fourth = shared.tile([P, 2 * HALF], BF16, name="fourth", align_bytes=64, offset=4 * N + 4 * HALF)
-        weave(first, 0, 256)
         scores(first, 0, 256)
         weave(third, 256, 384)
         weave(fourth, 384, 512)

@@ -53,9 +53,9 @@ def tile_attend_kv_append256_sink_kernel(tc, qT, kT, vT, new_kT, new_vT, vs, sin
             nc.sync.dma_start(kpool[t][:], kT_v[:, t, :])
             if t > 0:
                 nc.sync.dma_start(newk[t][:], newk_v[:, t, :])
-        nc.sync.dma_start(q_raw[:], qT.rearrange("b (p t) q -> p (b t) q", t=4))
         nc.sync.dma_start(newv[:], new_vT)
         nc.sync.dma_start(vpool[:], vT)
+        nc.sync.dma_start(q_raw[:], qT.rearrange("b (p t) q -> p (b t) q", t=4))
 
         ident = held.tile([P, P], F32, name="ident")
         make_identity(nc, ident[:])
@@ -88,13 +88,10 @@ def tile_attend_kv_append256_sink_kernel(tc, qT, kT, vT, new_kT, new_vT, vs, sin
         pairs = held.tile([P, 2, HALF, 2], BF16, name="pairs", align_bytes=64)
         for t in range(4):
             scatter("vector" if t == 0 else "scalar", kpool[t], newk[t])
-            if t == 0:
-                vs_col = held.tile([P, 4], F32, name="vs_col", tag="newk0")
-                nc.vector.tensor_copy(vs_col[:], vs_ps[:, :, P - 1])
             gather("vector", first[:, t::4], kpool[t], 0, HALF)
             gather("vector", pairs[:, t // 2, :, t % 2], kpool[t], HALF, N)
 
-        q_b = held.tile([P, NQ * 4], BF16, name="q_b", align_bytes=64)
+        q_b = held.tile([P, NQ * 4], BF16, name="q_b", tag="q_b", align_bytes=64)
         nc.gpsimd.tensor_copy(q_b[:].rearrange("p (q t) -> p q t", t=4), q_raw[:].rearrange("p t q -> p q t"))
         q_c = held.tile([P, NQ], U32, name="q_c", align_bytes=64)
         q_s = held.tile([P, NQ], U8, name="q_s", align_bytes=64)
@@ -124,6 +121,8 @@ def tile_attend_kv_append256_sink_kernel(tc, qT, kT, vT, new_kT, new_vT, vs, sin
         weave(third, 256, 384)
         weave(fourth, 384, 512)
         scores(third, 256, 384)
+        vs_col = held.tile([P, 4], F32, name="vs_col", tag="q_b", align_bytes=64)
+        nc.vector.tensor_copy(vs_col[:], vs_ps[:, :, P - 1])
         scores(fourth, 384, 512)
 
         negm = held.tile([P, 1], F32, name="negm")

@@ -20,6 +20,7 @@ AXIS_X = mybir.AxisListType.X
 P = 128
 N, T, D, DV, NQ, NEW = 512, 1024, 512, 128, 128, 256
 HALF = N // 2
+V_SCALAR = 448
 FLOPS = 2 * NQ * N * (D + DV)
 
 
@@ -98,9 +99,9 @@ def tile_attend_kv_append256_sink_kernel(tc, qT, kT, vT, new_kT, new_vT, vs, sin
         nc.vector.quantize_mx(out=q_c[:].bitcast(FP8X4), scales=q_s[:], in_=q_b[:])
 
 
-        v_q = held.tile([P, N], BF16, name="v_q", align_bytes=64)
+        v_q = shared.tile([P, N], BF16, name="v_q", align_bytes=64, offset=6 * N + 64)
         scatter("scalar", vpool, newv)
-        gather("scalar", v_q[:], vpool, 0, N)
+        gather("scalar", v_q[:, :V_SCALAR], vpool, 0, V_SCALAR)
 
         k_c = shared.tile([P, N], U32, name="k_c", align_bytes=64, offset=0)
         k_s = held.tile([P, N], U8, name="k_s", align_bytes=64)
@@ -115,15 +116,16 @@ def tile_attend_kv_append256_sink_kernel(tc, qT, kT, vT, new_kT, new_vT, vs, sin
             nc.vector.quantize_mx(out=k_c[:, c].bitcast(FP8X4), scales=k_s[:, c], in_=k_in[:])
             nc.tensor.matmul_mx(score[lo // HALF][:, lo % HALF : lo % HALF + hi - lo], lhsT=q_c[:].bitcast(FP8X4), lhsT_scale=q_s[:], rhs=k_c[:, c].bitcast(FP8X4), rhs_scale=k_s[:, c], start=True, stop=True)
 
-        third = shared.tile([P, 2 * HALF], BF16, name="third", align_bytes=64, offset=4 * N)
-        fourth = shared.tile([P, 2 * HALF], BF16, name="fourth", align_bytes=64, offset=4 * N + 4 * HALF)
+        third = shared.tile([P, 2 * HALF], BF16, name="third", align_bytes=64, offset=4 * N + 64)
+        fourth = held.tile([P, 2 * HALF], BF16, name="fourth", tag="q_b", align_bytes=64)
         scores(first, 0, 256)
         weave(third, 256, 384)
         weave(fourth, 384, 512)
         scores(third, 256, 384)
-        vs_col = held.tile([P, 4], F32, name="vs_col", tag="q_b", align_bytes=64)
+        vs_col = shared.tile([P, 4], F32, name="vs_col", align_bytes=64, offset=4 * N)
         nc.vector.tensor_copy(vs_col[:], vs_ps[:, :, P - 1])
         scores(fourth, 384, 512)
+        gather("vector", v_q[:, V_SCALAR:], vpool, V_SCALAR, N)
 
         negm = held.tile([P, 1], F32, name="negm")
         neg_score = held.tile([P, 4, P], F32, name="neg_score")

@@ -11,11 +11,9 @@ U16 = mybir.dt.uint16
 U8 = mybir.dt.uint8
 FP8X4 = mybir.dt.float8_e4m3fn_x4
 MULT = mybir.AluOpType.mult
-ADD = mybir.AluOpType.add
 MIN = mybir.AluOpType.min
 EXP = mybir.ActivationFunctionType.Exp
 COPY = mybir.ActivationFunctionType.Copy
-AXIS_X = mybir.AxisListType.X
 
 P = 128
 N, T, D, DV, NQ, NEW = 512, 1024, 512, 128, 128, 256
@@ -139,22 +137,21 @@ def tile_attend_kv_append256_sink_kernel(tc, qT, kT, vT, new_kT, new_vT, vs, sin
         v_b = held.tile([P, DV * 4], BF16, name="v_b", tag="v_b", align_bytes=64)
         nc.vector.tensor_copy(v_b[:].bitcast(F32).rearrange("p (e u) -> p e u", u=2), v_ps[:].rearrange("p u e -> p e u"))
 
-        p_sb = held.tile([P, 4, P], F32, name="p_sb")
-        l_ab = held.tile([P, 5], F32, name="l_ab")
+        p_sb = held.tile([P, N + 1], F32, name="p_sb")
         for t in range(4):
-            nc.scalar.activation(p_sb[:, t, :], neg_score[:, t, :], EXP, bias=negm[:], scale=-1.0, accum_out=l_ab[:, t : t + 1])
+            nc.scalar.activation(p_sb[:, t * P : (t + 1) * P], neg_score[:, t, :], EXP, bias=negm[:], scale=-1.0)
 
         v_c = held.tile([P, DV], U32, name="v_c", align_bytes=64)
         v_s = held.tile([P, DV], U8, name="v_s", align_bytes=64)
         nc.vector.quantize_mx(out=v_c[:].bitcast(FP8X4), scales=v_s[:], in_=v_b[:])
 
-        w_b = held.tile([P, NQ, 4], BF16, name="w_b", align_bytes=64)
+        w_b = held.tile([P, NQ, 4], BF16, name="w_b", tag="w_b", align_bytes=64)
         w_c = held.tile([P, NQ], U32, name="w_c", align_bytes=64)
         w_s = held.tile([P, NQ], U8, name="w_s", align_bytes=64)
         for h in range(2):
             p_ps = psum.tile([P, 2, NQ], F32, name=f"p_ps{h}")
             for t in range(2):
-                nc.tensor.transpose(p_ps[:, t, :], p_sb[:, 2 * h + t, :], ident[:])
+                nc.tensor.transpose(p_ps[:, t, :], p_sb[:, (2 * h + t) * P : (2 * h + t + 1) * P], ident[:])
             for c in ((slice(0, NQ),), (slice(0, NQ // 2), slice(NQ // 2, NQ)))[h]:
                 nc.vector.tensor_tensor(
                     w_b[:, c, 2 * h : 2 * h + 2],
@@ -169,10 +166,11 @@ def tile_attend_kv_append256_sink_kernel(tc, qT, kT, vT, new_kT, new_vT, vs, sin
         y_ps = psum.tile([P, DV], F32, name="y_ps")
         nc.tensor.matmul_mx(y_ps[:], lhsT=w_c[:].bitcast(FP8X4), lhsT_scale=w_s[:], rhs=v_c[:].bitcast(FP8X4), rhs_scale=v_s[:], start=True, stop=True)
 
-        nc.scalar.activation(l_ab[:, 4:5], negsink[:], EXP, bias=negm[:], scale=-1.0)
+        nc.scalar.activation(p_sb[:, N:], negsink[:], EXP, bias=negm[:], scale=-1.0)
         l_0 = held.tile([P, 1], F32, name="l_0")
-        nc.vector.tensor_reduce(l_0[:], l_ab[:], AXIS_X, ADD)
-        r_l = held.tile([P, 1], F32, name="r_l")
+        p_summed = held.tile([P, N + 1], F32, name="p_summed")
+        nc.scalar.activation(p_summed[:], p_sb[:], COPY, accum_out=l_0[:])
+        r_l = held.tile([P, 1], F32, name="r_l", tag="w_b", align_bytes=64)
         nc.vector.reciprocal(r_l[:], l_0[:])
 
         y_sb = held.tile([P, DV], F32, name="y_sb")

@@ -148,15 +148,15 @@ def tile_attend_kv_append256_sink_kernel(tc, qT, kT, vT, new_kT, new_vT, vs, sin
         w_b = held.tile([P, NQ, 4], BF16, name="w_b", tag="w_b", align_bytes=64)
         w_c = held.tile([P, NQ], U32, name="w_c", align_bytes=64)
         w_s = held.tile([P, NQ], U8, name="w_s", align_bytes=64)
-        for h in range(2):
-            p_ps = psum.tile([P, 2, NQ], F32, name=f"p_ps{h}")
-            for t in range(2):
-                nc.tensor.transpose(p_ps[:, t, :], p_sb[:, (2 * h + t) * P : (2 * h + t + 1) * P], ident[:])
-            for c in ((slice(0, NQ),), (slice(0, NQ // 2), slice(NQ // 2, NQ)))[h]:
+        for lo, hi, pieces in ((0, 1, (slice(0, NQ),)), (1, 4, (slice(0, NQ // 2), slice(NQ // 2, NQ)))):
+            p_ps = psum.tile([P, hi - lo, NQ], F32, name=f"p_ps{lo}")
+            for t in range(lo, hi):
+                nc.tensor.transpose(p_ps[:, t - lo, :], p_sb[:, t * P : (t + 1) * P], ident[:])
+            for c in pieces:
                 nc.vector.tensor_tensor(
-                    w_b[:, c, 2 * h : 2 * h + 2],
+                    w_b[:, c, lo:hi],
                     p_ps[:, :, c].rearrange("s t q -> s q t"),
-                    vs_col[:, 2 * h : 2 * h + 2].unsqueeze(1).to_broadcast([P, c.stop - c.start, 2]),
+                    vs_col[:, lo:hi].unsqueeze(1).to_broadcast([P, c.stop - c.start, hi - lo]),
                     MULT,
                 )
         for h in range(2):

@@ -18,7 +18,8 @@ COPY = mybir.ActivationFunctionType.Copy
 P = 128
 N, T, D, DV, NQ, NEW = 512, 1024, 512, 128, 128, 256
 HALF = N // 2
-V_SCALAR = 448
+QUARTER = N // 4
+PLANE = 4 * (NEW + T)
 FLOPS = 2 * NQ * N * (D + DV)
 
 
@@ -27,15 +28,16 @@ def tile_attend_kv_append256_sink_kernel(tc, qT, kT, vT, new_kT, new_vT, vs, sin
     with ExitStack() as ctx:
         held = ctx.enter_context(tc.tile_pool(name="held", bufs=1))
         shared = ctx.enter_context(tc.tile_pool(name="shared", bufs=1))
+        planes = ctx.enter_context(tc.tile_pool(name="planes", bufs=1))
         psum = ctx.enter_context(tc.psum_pool(name="psum", bufs=1))
 
         slots_sb = held.tile([P, NEW // 16], U16, name="slots_sb")
         offs_sb = held.tile([P, N // 16], U16, name="offs_sb")
         newv = held.tile([P, NEW], F32, name="newv")
         vpool = held.tile([P, T], F32, name="vpool")
-        newk = [held.tile([P, NEW], F32, name=f"newk{t}", tag=f"newk{t}") for t in range(4)]
-        kpool = [held.tile([P, T], F32, name=f"kpool{t}", tag=f"kpool{t}", align_bytes=64) for t in range(4)]
-        q_raw = shared.tile([P, 4, NQ], F32, name="q_raw", offset=4 * N - 64)
+        newk = [planes.tile([P, NEW], F32, name=f"newk{t}", tag=f"newk{t}", align_bytes=64, offset=t * PLANE) for t in range(4)]
+        kpool = [planes.tile([P, T], F32, name=f"kpool{t}", tag=f"kpool{t}", align_bytes=64, offset=t * PLANE + 4 * NEW) for t in range(4)]
+        q_raw = shared.tile([P, 4, NQ], F32, name="q_raw", offset=4 * N)
         vs_sb = held.tile([P, T], F32, name="vs_sb")
         sink_row = held.tile([P, NQ], F32, name="sink_row")
 
@@ -52,124 +54,116 @@ def tile_attend_kv_append256_sink_kernel(tc, qT, kT, vT, new_kT, new_vT, vs, sin
             nc.sync.dma_start(kpool[t][:], kT_v[:, t, :])
             if t > 0:
                 nc.sync.dma_start(newk[t][:], newk_v[:, t, :])
+        nc.sync.dma_start(q_raw[:], qT.rearrange("b (p t) q -> p (b t) q", t=4))
         nc.sync.dma_start(newv[:], new_vT)
         nc.sync.dma_start(vpool[:], vT)
-        nc.sync.dma_start(q_raw[:], qT.rearrange("b (p t) q -> p (b t) q", t=4))
 
         ident = held.tile([P, P], F32, name="ident")
         make_identity(nc, ident[:])
 
-        def scatter(engine, pool_tile, new_tile):
-            if engine == "vector":
-                nc.vector.tensor_copy(pool_tile[:].indirect(slots_sb[:]), new_tile[:])
-            else:
-                nc.scalar.activation(pool_tile[:].indirect(slots_sb[:]), new_tile[:], COPY)
+        def listed(pool_tile, lo, hi):
+            return pool_tile[:].indirect(offs_sb[:, lo // 16 : hi // 16])
 
-        def gather(engine, dst, pool_tile, lo, hi):
-            window = pool_tile[:].indirect(offs_sb[:, lo // 16 : hi // 16])
-            if engine == "vector":
-                nc.vector.tensor_copy(dst, window)
-            else:
-                nc.scalar.activation(dst, window, COPY)
-
-        negsink = held.tile([P, 1], F32, name="negsink")
-        sink_ps = psum.tile([P, P], F32, name="sink_ps")
-        nc.tensor.transpose(sink_ps[:], sink_row[:], ident[:])
-        nc.scalar.activation(negsink[:], sink_ps[:, P - 1 :], COPY, scale=-1.0)
+        sink_ps = psum.tile([P, 2, P], F32, name="sink_ps", tag="sink_then_values")
+        nc.tensor.transpose(sink_ps[:, 0, :], sink_row[:], ident[:])
 
         vs_g = held.tile([P, N], F32, name="vs_g")
-        gather("scalar", vs_g[:], vs_sb, 0, N)
+        nc.scalar.activation(vs_g[:], listed(vs_sb, 0, N), COPY)
         vs_ps = psum.tile([P, 4, P], F32, name="vs_ps")
         for t in range(4):
             nc.tensor.transpose(vs_ps[:, t, :], vs_g[:, t::4], ident[:])
 
         first = held.tile([P, 4 * HALF], BF16, name="first", align_bytes=64)
         pairs = held.tile([P, 2, HALF, 2], BF16, name="pairs", align_bytes=64)
-        for t in range(4):
-            scatter("vector" if t == 0 else "scalar", kpool[t], newk[t])
-            gather("vector", first[:, t::4], kpool[t], 0, HALF)
-            gather("vector", pairs[:, t // 2, :, t % 2], kpool[t], HALF, N)
+        nc.vector.tensor_copy(kpool[0][:].indirect(slots_sb[:]), newk[0][:])
+        for t in range(1, 4):
+            nc.scalar.activation(kpool[t][:].indirect(slots_sb[:]), newk[t][:], COPY)
+        for t in range(3):
+            nc.vector.tensor_copy(first[:, t::4], listed(kpool[t], 0, HALF))
+            nc.vector.tensor_copy(pairs[:, t // 2, :, t % 2], listed(kpool[t], HALF, N))
+        nc.vector.tensor_copy(pairs[:, 1, :, 1], listed(kpool[3], HALF, N))
+        negsink = planes.tile([P, 16], F32, name="negsink", offset=3 * PLANE - 32)
+        nc.scalar.activation(negsink[:, :1], sink_ps[:, 0, P - 1 :], COPY, scale=-1.0)
+        for lo in (0, QUARTER):
+            nc.scalar.activation(first[:, 4 * lo + 3 : 4 * (lo + QUARTER) : 4], listed(kpool[3], lo, lo + QUARTER), COPY)
+        nc.scalar.activation(vpool[:].indirect(slots_sb[:]), newv[:], COPY)
 
-        q_b = held.tile([P, NQ * 4], BF16, name="q_b", tag="q_b", align_bytes=64)
+        q_b = held.tile([P, NQ * 4], BF16, name="q_b", align_bytes=64)
         nc.gpsimd.tensor_copy(q_b[:].rearrange("p (q t) -> p q t", t=4), q_raw[:].rearrange("p t q -> p q t"))
         q_c = held.tile([P, NQ], U32, name="q_c", align_bytes=64)
         q_s = held.tile([P, NQ], U8, name="q_s", align_bytes=64)
         nc.vector.quantize_mx(out=q_c[:].bitcast(FP8X4), scales=q_s[:], in_=q_b[:])
 
-
-        v_q = shared.tile([P, N], BF16, name="v_q", align_bytes=64, offset=6 * N + 64)
-        scatter("scalar", vpool, newv)
-        gather("scalar", v_q[:, :V_SCALAR], vpool, 0, V_SCALAR)
-
-        k_c = shared.tile([P, N], U32, name="k_c", align_bytes=64, offset=0)
+        k_c = shared.tile([P, N], U32, name="k_c", align_bytes=64, offset=64)
         k_s = held.tile([P, N], U8, name="k_s", align_bytes=64)
-        score = [psum.tile([P, HALF], F32, name=f"score{h}", tag=f"score{h}") for h in range(2)]
+        vs_col = shared.tile([P, 4], F32, name="vs_col", align_bytes=64, offset=4 * N + 64)
+        third = shared.tile([P, 4 * QUARTER], BF16, name="third", align_bytes=64, offset=4 * N + 128)
+        fourth = shared.tile([P, 4 * QUARTER], BF16, name="fourth", align_bytes=64, offset=6 * N + 128)
+        score_head = psum.tile([P, QUARTER], F32, name="score_head")
+        score_rest = psum.tile([P, N - QUARTER], F32, name="score_rest")
 
-        def weave(k_in, lo, hi):
+        def weave(k_in, quarter):
             words = pairs[:].rearrange("p u n e -> p (u n e)").bitcast(I32).rearrange("p (u n) -> p n u", u=2)
-            nc.vector.tensor_copy(k_in[:].bitcast(I32).rearrange("p (n u) -> p n u", u=2), words[:, lo % HALF : lo % HALF + hi - lo, :])
+            lo = quarter * QUARTER - HALF
+            nc.vector.tensor_copy(k_in[:].bitcast(I32).rearrange("p (n u) -> p n u", u=2), words[:, lo : lo + QUARTER, :])
 
-        def scores(k_in, lo, hi):
-            c = slice(lo, hi)
-            nc.vector.quantize_mx(out=k_c[:, c].bitcast(FP8X4), scales=k_s[:, c], in_=k_in[:])
-            nc.tensor.matmul_mx(score[lo // HALF][:, lo % HALF : lo % HALF + hi - lo], lhsT=q_c[:].bitcast(FP8X4), lhsT_scale=q_s[:], rhs=k_c[:, c].bitcast(FP8X4), rhs_scale=k_s[:, c], start=True, stop=True)
+        def scores(k_in, quarter):
+            c = slice(quarter * QUARTER, (quarter + 1) * QUARTER)
+            dst = score_head[:] if quarter == 0 else score_rest[:, c.start - QUARTER : c.stop - QUARTER]
+            nc.vector.quantize_mx(out=k_c[:, c].bitcast(FP8X4), scales=k_s[:, c], in_=k_in)
+            nc.tensor.matmul_mx(dst, lhsT=q_c[:].bitcast(FP8X4), lhsT_scale=q_s[:], rhs=k_c[:, c].bitcast(FP8X4), rhs_scale=k_s[:, c], start=True, stop=True)
 
-        third = shared.tile([P, 2 * HALF], BF16, name="third", align_bytes=64, offset=4 * N + 64)
-        fourth = held.tile([P, 2 * HALF], BF16, name="fourth", tag="q_b", align_bytes=64)
-        scores(first, 0, 256)
-        weave(third, 256, 384)
-        weave(fourth, 384, 512)
-        scores(third, 256, 384)
-        vs_col = shared.tile([P, 4], F32, name="vs_col", align_bytes=64, offset=4 * N)
+        scores(first[:, : 4 * QUARTER], 0)
+        weave(third, 2)
+        weave(fourth, 3)
+        scores(first[:, 4 * QUARTER :], 1)
+        scores(third[:], 2)
+        scores(fourth[:], 3)
         nc.vector.tensor_copy(vs_col[:], vs_ps[:, :, P - 1])
-        scores(fourth, 384, 512)
-        gather("vector", v_q[:, V_SCALAR:], vpool, V_SCALAR, N)
 
         negm = held.tile([P, 1], F32, name="negm")
+        negm_head = held.tile([P, 1], F32, name="negm_head")
         neg_score = held.tile([P, 4, P], F32, name="neg_score")
-        negm_0 = held.tile([P, 1], F32, name="negm_0", tag="v_b", align_bytes=64)
-        nc.vector.tensor_scalar(neg_score[:, :, : P // 2], score[0][:].rearrange("q (s t) -> q t s", t=4), -1.0, negsink[:], op0=MULT, op1=MIN, accum_out=negm_0[:])
-        nc.vector.tensor_scalar(neg_score[:, :, P // 2 :], score[1][:].rearrange("q (s t) -> q t s", t=4), -1.0, negm_0[:], op0=MULT, op1=MIN, accum_out=negm[:])
+        nc.vector.tensor_scalar(neg_score[:, :, : P // 4], score_head[:].rearrange("q (s t) -> q t s", t=4), -1.0, negsink[:, :1], op0=MULT, op1=MIN, accum_out=negm_head[:])
+        nc.vector.tensor_scalar(neg_score[:, :, P // 4 :], score_rest[:].rearrange("q (s t) -> q t s", t=4), -1.0, negm_head[:], op0=MULT, op1=MIN, accum_out=negm[:])
 
-        v_ps = psum.tile([P, 2, DV], F32, name="v_ps", tag="score0")
-        for u in range(2):
-            nc.tensor.transpose(v_ps[:, u, :], v_q[:].bitcast(F32)[:, u::2], ident[:])
-        v_b = held.tile([P, DV * 4], BF16, name="v_b", tag="v_b", align_bytes=64)
-        nc.vector.tensor_copy(v_b[:].bitcast(F32).rearrange("p (e u) -> p e u", u=2), v_ps[:].rearrange("p u e -> p e u"))
+        v_q = shared.tile([P, N], BF16, name="v_q", align_bytes=64, offset=64)
+        nc.vector.tensor_copy(v_q[:].rearrange("d (u s e) -> d s u e", u=2, e=2), listed(vpool, 0, N))
 
         p_sb = held.tile([P, N + 1], F32, name="p_sb")
+        p_ps = psum.tile([P, 4, NQ], F32, name="p_ps")
         for t in range(4):
             nc.scalar.activation(p_sb[:, t * P : (t + 1) * P], neg_score[:, t, :], EXP, bias=negm[:], scale=-1.0)
+            nc.tensor.transpose(p_ps[:, t, :], p_sb[:, t * P : (t + 1) * P], ident[:])
+        nc.scalar.activation(p_sb[:, N:], sink_ps[:, 0, P - 1 :], EXP, bias=negm[:])
 
-        v_c = held.tile([P, DV], U32, name="v_c", align_bytes=64)
-        v_s = held.tile([P, DV], U8, name="v_s", align_bytes=64)
-        nc.vector.quantize_mx(out=v_c[:].bitcast(FP8X4), scales=v_s[:], in_=v_b[:])
+        v_ps = psum.tile([P, 2, DV], F32, name="v_ps", tag="sink_then_values")
+        for u in range(2):
+            nc.tensor.transpose(v_ps[:, u, :], v_q[:].bitcast(F32)[:, u * P : (u + 1) * P], ident[:])
 
         w_b = held.tile([P, NQ, 4], BF16, name="w_b", tag="w_b", align_bytes=64)
         w_c = held.tile([P, NQ], U32, name="w_c", align_bytes=64)
         w_s = held.tile([P, NQ], U8, name="w_s", align_bytes=64)
-        for lo, hi, pieces in ((0, 1, (slice(0, NQ),)), (1, 4, (slice(0, NQ // 2), slice(NQ // 2, NQ)))):
-            p_ps = psum.tile([P, hi - lo, NQ], F32, name=f"p_ps{lo}")
-            for t in range(lo, hi):
-                nc.tensor.transpose(p_ps[:, t - lo, :], p_sb[:, t * P : (t + 1) * P], ident[:])
-            for c in pieces:
-                nc.vector.tensor_tensor(
-                    w_b[:, c, lo:hi],
-                    p_ps[:, :, c].rearrange("s t q -> s q t"),
-                    vs_col[:, lo:hi].unsqueeze(1).to_broadcast([P, c.stop - c.start, hi - lo]),
-                    MULT,
-                )
-        for h in range(2):
-            c = slice(h * NQ // 2, (h + 1) * NQ // 2)
+        halves = [slice(h * NQ // 2, (h + 1) * NQ // 2) for h in range(2)]
+        for c in halves:
+            nc.vector.tensor_tensor(w_b[:, c, :], p_ps[:, :, c].rearrange("s t q -> s q t"), vs_col[:].unsqueeze(1).to_broadcast([P, NQ // 2, 4]), MULT)
+
+        l_0 = held.tile([P, 1], F32, name="l_0")
+        p_summed = held.tile([P, N + 1], F32, name="p_summed")
+        nc.scalar.activation(p_summed[:], p_sb[:], COPY, accum_out=l_0[:])
+
+        v_b = held.tile([P, DV * 4], BF16, name="v_b", align_bytes=64)
+        nc.scalar.copy(v_b[:].bitcast(F32).rearrange("p (e u) -> p e u", u=2), v_ps[:].rearrange("p u e -> p e u"))
+
+        for c in halves:
             nc.vector.quantize_mx(out=w_c[:, c].bitcast(FP8X4), scales=w_s[:, c], in_=w_b[:, c, :].rearrange("p q t -> p (q t)"))
+        v_c = held.tile([P, DV], U32, name="v_c", align_bytes=64)
+        v_s = held.tile([P, DV], U8, name="v_s", align_bytes=64)
+        nc.vector.quantize_mx(out=v_c[:].bitcast(FP8X4), scales=v_s[:], in_=v_b[:])
 
         y_ps = psum.tile([P, DV], F32, name="y_ps")
         nc.tensor.matmul_mx(y_ps[:], lhsT=w_c[:].bitcast(FP8X4), lhsT_scale=w_s[:], rhs=v_c[:].bitcast(FP8X4), rhs_scale=v_s[:], start=True, stop=True)
 
-        nc.scalar.activation(p_sb[:, N:], negsink[:], EXP, bias=negm[:], scale=-1.0)
-        l_0 = held.tile([P, 1], F32, name="l_0")
-        p_summed = held.tile([P, N + 1], F32, name="p_summed")
-        nc.scalar.activation(p_summed[:], p_sb[:], COPY, accum_out=l_0[:])
         r_l = held.tile([P, 1], F32, name="r_l", tag="w_b", align_bytes=64)
         nc.vector.reciprocal(r_l[:], l_0[:])
 

@@ -20,6 +20,7 @@ N, T, D, DV, NQ, NEW = 512, 1024, 512, 128, 128, 256
 HALF = N // 2
 QUARTER = N // 4
 PLANE = 4 * (NEW + T)
+V_SCALAR = 64
 FLOPS = 2 * NQ * N * (D + DV)
 
 
@@ -128,13 +129,16 @@ def tile_attend_kv_append256_sink_kernel(tc, qT, kT, vT, new_kT, new_vT, vs, sin
         nc.vector.tensor_scalar(neg_score[:, :, P // 4 :], score_rest[:].rearrange("q (s t) -> q t s", t=4), -1.0, negm_head[:], op0=MULT, op1=MIN, accum_out=negm[:])
 
         v_q = shared.tile([P, N], BF16, name="v_q", align_bytes=64, offset=64)
-        nc.vector.tensor_copy(v_q[:].rearrange("d (u s e) -> d s u e", u=2, e=2), listed(vpool, 0, N))
+        v_dealt = v_q[:].rearrange("d (u s e) -> d s u e", u=2, e=2)
+        nc.scalar.activation(v_dealt[:, : V_SCALAR // 4], listed(vpool, 0, V_SCALAR), COPY)
+        nc.vector.tensor_copy(v_dealt[:, V_SCALAR // 4 :], listed(vpool, V_SCALAR, N))
 
         p_sb = held.tile([P, N + 1], F32, name="p_sb")
-        p_ps = psum.tile([P, 4, NQ], F32, name="p_ps")
+        p_head = psum.tile([P, 1, NQ], F32, name="p_head")
+        p_rest = psum.tile([P, 3, NQ], F32, name="p_rest")
         for t in range(4):
             nc.scalar.activation(p_sb[:, t * P : (t + 1) * P], neg_score[:, t, :], EXP, bias=negm[:], scale=-1.0)
-            nc.tensor.transpose(p_ps[:, t, :], p_sb[:, t * P : (t + 1) * P], ident[:])
+            nc.tensor.transpose(p_rest[:, t - 1, :] if t else p_head[:, 0, :], p_sb[:, t * P : (t + 1) * P], ident[:])
         nc.scalar.activation(p_sb[:, N:], sink_ps[:, 0, P - 1 :], EXP, bias=negm[:])
 
         v_ps = psum.tile([P, 2, DV], F32, name="v_ps", tag="sink_then_values")
@@ -145,21 +149,24 @@ def tile_attend_kv_append256_sink_kernel(tc, qT, kT, vT, new_kT, new_vT, vs, sin
         w_c = held.tile([P, NQ], U32, name="w_c", align_bytes=64)
         w_s = held.tile([P, NQ], U8, name="w_s", align_bytes=64)
         halves = [slice(h * NQ // 2, (h + 1) * NQ // 2) for h in range(2)]
+        nc.vector.tensor_tensor(w_b[:, :, :1], p_head[:].rearrange("s t q -> s q t"), vs_col[:, :1].unsqueeze(1).to_broadcast([P, NQ, 1]), MULT)
         for c in halves:
-            nc.vector.tensor_tensor(w_b[:, c, :], p_ps[:, :, c].rearrange("s t q -> s q t"), vs_col[:].unsqueeze(1).to_broadcast([P, NQ // 2, 4]), MULT)
+            nc.vector.tensor_tensor(w_b[:, c, 1:], p_rest[:, :, c].rearrange("s t q -> s q t"), vs_col[:, 1:].unsqueeze(1).to_broadcast([P, NQ // 2, 3]), MULT)
 
         l_0 = held.tile([P, 1], F32, name="l_0")
         p_summed = held.tile([P, N + 1], F32, name="p_summed")
         nc.scalar.activation(p_summed[:], p_sb[:], COPY, accum_out=l_0[:])
 
         v_b = held.tile([P, DV * 4], BF16, name="v_b", align_bytes=64)
-        nc.scalar.copy(v_b[:].bitcast(F32).rearrange("p (e u) -> p e u", u=2), v_ps[:].rearrange("p u e -> p e u"))
+        for c in halves:
+            nc.scalar.copy(v_b[:].bitcast(F32).rearrange("p (e u) -> p e u", u=2)[:, c, :], v_ps[:, :, c].rearrange("p u e -> p e u"))
 
         for c in halves:
             nc.vector.quantize_mx(out=w_c[:, c].bitcast(FP8X4), scales=w_s[:, c], in_=w_b[:, c, :].rearrange("p q t -> p (q t)"))
         v_c = held.tile([P, DV], U32, name="v_c", align_bytes=64)
         v_s = held.tile([P, DV], U8, name="v_s", align_bytes=64)
-        nc.vector.quantize_mx(out=v_c[:].bitcast(FP8X4), scales=v_s[:], in_=v_b[:])
+        for c in halves:
+            nc.vector.quantize_mx(out=v_c[:, c].bitcast(FP8X4), scales=v_s[:, c], in_=v_b[:, 4 * c.start : 4 * c.stop])
 
         y_ps = psum.tile([P, DV], F32, name="y_ps")
         nc.tensor.matmul_mx(y_ps[:], lhsT=w_c[:].bitcast(FP8X4), lhsT_scale=w_s[:], rhs=v_c[:].bitcast(FP8X4), rhs_scale=v_s[:], start=True, stop=True)

@@ -34,11 +34,11 @@ def tile_attend_kv_append256_sink_kernel(tc, qT, kT, vT, new_kT, new_vT, vs, sin
 
         slots_sb = held.tile([P, NEW // 16], U16, name="slots_sb")
         offs_sb = held.tile([P, N // 16], U16, name="offs_sb")
-        newv = held.tile([P, NEW], F32, name="newv")
-        vpool = held.tile([P, T], F32, name="vpool")
-        newk = [planes.tile([P, NEW], F32, name=f"newk{t}", tag=f"newk{t}", align_bytes=64, offset=t * PLANE) for t in range(4)]
-        kpool = [planes.tile([P, T], F32, name=f"kpool{t}", tag=f"kpool{t}", align_bytes=64, offset=t * PLANE + 4 * NEW) for t in range(4)]
-        q_raw = shared.tile([P, 4, NQ], F32, name="q_raw", offset=4 * N)
+        newv = held.tile([P, NEW], F32, name="newv", align_bytes=256)
+        vpool = held.tile([P, T], F32, name="vpool", align_bytes=256)
+        newk = [planes.tile([P, NEW], F32, name=f"newk{t}", tag=f"newk{t}", align_bytes=256, offset=t * PLANE) for t in range(4)]
+        kpool = [planes.tile([P, T], F32, name=f"kpool{t}", tag=f"kpool{t}", align_bytes=256, offset=t * PLANE + 4 * NEW) for t in range(4)]
+        q_raw = shared.tile([P, 4, NQ], F32, name="q_raw", align_bytes=256, offset=4 * N)
         vs_sb = held.tile([P, T], F32, name="vs_sb")
         sink_row = held.tile([P, NQ], F32, name="sink_row")
 

@@ -45,7 +45,6 @@ def tile_attend_kv_append256_sink_kernel(tc, qT, kT, vT, new_kT, new_vT, vs, sin
         kT_v = kT.rearrange("(p t) n -> p t n", t=4)
         newk_v = new_kT.rearrange("(p t) n -> p t n", t=4)
         nc.scalar.dma_start(vs_sb[P - 1 : P, :], vs[0:1, :])
-        nc.scalar.dma_start(sink_row[P - 1 : P, :], sink.rearrange("b q o -> (b o) q"))
         nc.vector.memset(vs_sb[: P - 1, :], 0.0)
         nc.scalar.activation(sink_row[: P - 1, :], vs_sb[: P - 1, :NQ], COPY)
         nc.sync.dma_start(newk[0][:], newk_v[:, 0, :])
@@ -53,6 +52,8 @@ def tile_attend_kv_append256_sink_kernel(tc, qT, kT, vT, new_kT, new_vT, vs, sin
         nc.sync.dma_start(slots_sb[:], slots)
         for t in range(4):
             nc.sync.dma_start(kpool[t][:], kT_v[:, t, :])
+            if t == 3:
+                nc.sync.dma_start(sink_row[P - 1 : P, :], sink.rearrange("b q o -> (b o) q"))
             if t > 0:
                 nc.sync.dma_start(newk[t][:], newk_v[:, t, :])
         nc.sync.dma_start(q_raw[:], qT.rearrange("b (p t) q -> p (b t) q", t=4))
@@ -82,7 +83,8 @@ def tile_attend_kv_append256_sink_kernel(tc, qT, kT, vT, new_kT, new_vT, vs, sin
         for t in range(3):
             nc.vector.tensor_copy(first[:, t::4], listed(kpool[t], 0, HALF))
             nc.vector.tensor_copy(pairs[:, t // 2, :, t % 2], listed(kpool[t], HALF, N))
-        nc.vector.tensor_copy(pairs[:, 1, :, 1], listed(kpool[3], HALF, N))
+        for lo in (0, QUARTER):
+            nc.vector.tensor_copy(pairs[:, 1, lo : lo + QUARTER, 1], listed(kpool[3], HALF + lo, HALF + lo + QUARTER))
         negsink = planes.tile([P, 16], F32, name="negsink", offset=3 * PLANE - 32)
         nc.scalar.activation(negsink[:, :1], sink_ps[:, 0, P - 1 :], COPY, scale=-1.0)
         for lo in (0, QUARTER):
@@ -114,11 +116,11 @@ def tile_attend_kv_append256_sink_kernel(tc, qT, kT, vT, new_kT, new_vT, vs, sin
             nc.vector.quantize_mx(out=k_c[:, c].bitcast(FP8X4), scales=k_s[:, c], in_=k_in)
             nc.tensor.matmul_mx(dst, lhsT=q_c[:].bitcast(FP8X4), lhsT_scale=q_s[:], rhs=k_c[:, c].bitcast(FP8X4), rhs_scale=k_s[:, c], start=True, stop=True)
 
-        scores(first[:, : 4 * QUARTER], 0)
         weave(third, 2)
+        scores(first[:, : 4 * QUARTER], 0)
         weave(fourth, 3)
-        scores(first[:, 4 * QUARTER :], 1)
         scores(third[:], 2)
+        scores(first[:, 4 * QUARTER :], 1)
         scores(fourth[:], 3)
         nc.vector.tensor_copy(vs_col[:], vs_ps[:, :, P - 1])
 

from contextlib import ExitStack

import concourse.mybir as mybir
from concourse.masks import make_identity

F32 = mybir.dt.float32
BF16 = mybir.dt.bfloat16
U32 = mybir.dt.uint32
I32 = mybir.dt.int32
U16 = mybir.dt.uint16
U8 = mybir.dt.uint8
FP8X4 = mybir.dt.float8_e4m3fn_x4
MULT = mybir.AluOpType.mult
MIN = mybir.AluOpType.min
EXP = mybir.ActivationFunctionType.Exp
COPY = mybir.ActivationFunctionType.Copy

P = 128
N, T, D, DV, NQ, NEW = 512, 1024, 512, 128, 128, 256
HALF = N // 2
QUARTER = N // 4
PLANE = 4 * (NEW + T)
V_SCALAR = 64
FLOPS = 2 * NQ * N * (D + DV)


def tile_attend_kv_append256_sink_kernel(tc, qT, kT, vT, new_kT, new_vT, vs, sink, offs, slots, out):
    nc = tc.nc
    with ExitStack() as ctx:
        held = ctx.enter_context(tc.tile_pool(name="held", bufs=1))
        shared = ctx.enter_context(tc.tile_pool(name="shared", bufs=1))
        planes = ctx.enter_context(tc.tile_pool(name="planes", bufs=1))
        psum = ctx.enter_context(tc.psum_pool(name="psum", bufs=1))

        slots_sb = held.tile([P, NEW // 16], U16, name="slots_sb")
        offs_sb = held.tile([P, N // 16], U16, name="offs_sb")
        newv = held.tile([P, NEW], F32, name="newv", align_bytes=256)
        vpool = held.tile([P, T], F32, name="vpool", align_bytes=256)
        newk = [planes.tile([P, NEW], F32, name=f"newk{t}", tag=f"newk{t}", align_bytes=256, offset=t * PLANE) for t in range(4)]
        kpool = [planes.tile([P, T], F32, name=f"kpool{t}", tag=f"kpool{t}", align_bytes=256, offset=t * PLANE + 4 * NEW) for t in range(4)]
        q_raw = shared.tile([P, 4, NQ], F32, name="q_raw", align_bytes=256, offset=4 * N)
        vs_sb = held.tile([P, T], F32, name="vs_sb")
        sink_row = held.tile([P, NQ], F32, name="sink_row")

        kT_v = kT.rearrange("(p t) n -> p t n", t=4)
        newk_v = new_kT.rearrange("(p t) n -> p t n", t=4)
        nc.scalar.dma_start(vs_sb[P - 1 : P, :], vs[0:1, :])
        nc.vector.memset(vs_sb[: P - 1, :], 0.0)
        nc.scalar.activation(sink_row[: P - 1, :], vs_sb[: P - 1, :NQ], COPY)
        nc.sync.dma_start(newk[0][:], newk_v[:, 0, :])
        nc.sync.dma_start(offs_sb[:], offs)
        nc.sync.dma_start(slots_sb[:], slots)
        for t in range(4):
            nc.sync.dma_start(kpool[t][:], kT_v[:, t, :])
            if t == 3:
                nc.sync.dma_start(sink_row[P - 1 : P, :], sink.rearrange("b q o -> (b o) q"))
            if t > 0:
                nc.sync.dma_start(newk[t][:], newk_v[:, t, :])
        nc.sync.dma_start(q_raw[:], qT.rearrange("b (p t) q -> p (b t) q", t=4))
        nc.sync.dma_start(newv[:], new_vT)
        nc.sync.dma_start(vpool[:], vT)

        ident = held.tile([P, P], F32, name="ident")
        make_identity(nc, ident[:])

        def listed(pool_tile, lo, hi):
            return pool_tile[:].indirect(offs_sb[:, lo // 16 : hi // 16])

        sink_ps = psum.tile([P, 2, P], F32, name="sink_ps", tag="sink_then_values")
        nc.tensor.transpose(sink_ps[:, 0, :], sink_row[:], ident[:])

        vs_g = held.tile([P, N], F32, name="vs_g")
        nc.scalar.activation(vs_g[:], listed(vs_sb, 0, N), COPY)
        vs_ps = psum.tile([P, 4, P], F32, name="vs_ps")
        for t in range(4):
            nc.tensor.transpose(vs_ps[:, t, :], vs_g[:, t::4], ident[:])

        first = held.tile([P, 4 * HALF], BF16, name="first", align_bytes=64)
        pairs = held.tile([P, 2, HALF, 2], BF16, name="pairs", align_bytes=64)
        nc.vector.tensor_copy(kpool[0][:].indirect(slots_sb[:]), newk[0][:])
        for t in range(1, 4):
            nc.scalar.activation(kpool[t][:].indirect(slots_sb[:]), newk[t][:], COPY)
        for t in range(3):
            nc.vector.tensor_copy(first[:, t::4], listed(kpool[t], 0, HALF))
            nc.vector.tensor_copy(pairs[:, t // 2, :, t % 2], listed(kpool[t], HALF, N))
        for lo in (0, QUARTER):
            nc.vector.tensor_copy(pairs[:, 1, lo : lo + QUARTER, 1], listed(kpool[3], HALF + lo, HALF + lo + QUARTER))
        negsink = planes.tile([P, 16], F32, name="negsink", offset=3 * PLANE - 32)
        nc.scalar.activation(negsink[:, :1], sink_ps[:, 0, P - 1 :], COPY, scale=-1.0)
        for lo in (0, QUARTER):
            nc.scalar.activation(first[:, 4 * lo + 3 : 4 * (lo + QUARTER) : 4], listed(kpool[3], lo, lo + QUARTER), COPY)
        nc.scalar.activation(vpool[:].indirect(slots_sb[:]), newv[:], COPY)

        q_b = held.tile([P, NQ * 4], BF16, name="q_b", align_bytes=64)
        nc.gpsimd.tensor_copy(q_b[:].rearrange("p (q t) -> p q t", t=4), q_raw[:].rearrange("p t q -> p q t"))
        q_c = held.tile([P, NQ], U32, name="q_c", align_bytes=64)
        q_s = held.tile([P, NQ], U8, name="q_s", align_bytes=64)
        nc.vector.quantize_mx(out=q_c[:].bitcast(FP8X4), scales=q_s[:], in_=q_b[:])

        k_c = shared.tile([P, N], U32, name="k_c", align_bytes=64, offset=64)
        k_s = held.tile([P, N], U8, name="k_s", align_bytes=64)
        vs_col = shared.tile([P, 4], F32, name="vs_col", align_bytes=64, offset=4 * N + 64)
        third = shared.tile([P, 4 * QUARTER], BF16, name="third", align_bytes=64, offset=4 * N + 128)
        fourth = shared.tile([P, 4 * QUARTER], BF16, name="fourth", align_bytes=64, offset=6 * N + 128)
        score_head = psum.tile([P, QUARTER], F32, name="score_head")
        score_rest = psum.tile([P, N - QUARTER], F32, name="score_rest")

        def weave(k_in, quarter):
            words = pairs[:].rearrange("p u n e -> p (u n e)").bitcast(I32).rearrange("p (u n) -> p n u", u=2)
            lo = quarter * QUARTER - HALF
            nc.vector.tensor_copy(k_in[:].bitcast(I32).rearrange("p (n u) -> p n u", u=2), words[:, lo : lo + QUARTER, :])

        def scores(k_in, quarter):
            c = slice(quarter * QUARTER, (quarter + 1) * QUARTER)
            dst = score_head[:] if quarter == 0 else score_rest[:, c.start - QUARTER : c.stop - QUARTER]
            nc.vector.quantize_mx(out=k_c[:, c].bitcast(FP8X4), scales=k_s[:, c], in_=k_in)
            nc.tensor.matmul_mx(dst, lhsT=q_c[:].bitcast(FP8X4), lhsT_scale=q_s[:], rhs=k_c[:, c].bitcast(FP8X4), rhs_scale=k_s[:, c], start=True, stop=True)

        weave(third, 2)
        scores(first[:, : 4 * QUARTER], 0)
        weave(fourth, 3)
        scores(third[:], 2)
        scores(first[:, 4 * QUARTER :], 1)
        scores(fourth[:], 3)
        nc.vector.tensor_copy(vs_col[:], vs_ps[:, :, P - 1])

        negm = held.tile([P, 1], F32, name="negm")
        negm_head = held.tile([P, 1], F32, name="negm_head")
        neg_score = held.tile([P, 4, P], F32, name="neg_score")
        nc.vector.tensor_scalar(neg_score[:, :, : P // 4], score_head[:].rearrange("q (s t) -> q t s", t=4), -1.0, negsink[:, :1], op0=MULT, op1=MIN, accum_out=negm_head[:])
        nc.vector.tensor_scalar(neg_score[:, :, P // 4 :], score_rest[:].rearrange("q (s t) -> q t s", t=4), -1.0, negm_head[:], op0=MULT, op1=MIN, accum_out=negm[:])

        v_q = shared.tile([P, N], BF16, name="v_q", align_bytes=64, offset=64)
        v_dealt = v_q[:].rearrange("d (u s e) -> d s u e", u=2, e=2)
        nc.scalar.activation(v_dealt[:, : V_SCALAR // 4], listed(vpool, 0, V_SCALAR), COPY)
        nc.vector.tensor_copy(v_dealt[:, V_SCALAR // 4 :], listed(vpool, V_SCALAR, N))

        p_sb = held.tile([P, N + 1], F32, name="p_sb")
        p_head = psum.tile([P, 1, NQ], F32, name="p_head")
        p_rest = psum.tile([P, 3, NQ], F32, name="p_rest")
        for t in range(4):
            nc.scalar.activation(p_sb[:, t * P : (t + 1) * P], neg_score[:, t, :], EXP, bias=negm[:], scale=-1.0)
            nc.tensor.transpose(p_rest[:, t - 1, :] if t else p_head[:, 0, :], p_sb[:, t * P : (t + 1) * P], ident[:])
        nc.scalar.activation(p_sb[:, N:], sink_ps[:, 0, P - 1 :], EXP, bias=negm[:])

        v_ps = psum.tile([P, 2, DV], F32, name="v_ps", tag="sink_then_values")
        for u in range(2):
            nc.tensor.transpose(v_ps[:, u, :], v_q[:].bitcast(F32)[:, u * P : (u + 1) * P], ident[:])

        w_b = held.tile([P, NQ, 4], BF16, name="w_b", tag="w_b", align_bytes=64)
        w_c = held.tile([P, NQ], U32, name="w_c", align_bytes=64)
        w_s = held.tile([P, NQ], U8, name="w_s", align_bytes=64)
        halves = [slice(h * NQ // 2, (h + 1) * NQ // 2) for h in range(2)]
        nc.vector.tensor_tensor(w_b[:, :, :1], p_head[:].rearrange("s t q -> s q t"), vs_col[:, :1].unsqueeze(1).to_broadcast([P, NQ, 1]), MULT)
        for c in halves:
            nc.vector.tensor_tensor(w_b[:, c, 1:], p_rest[:, :, c].rearrange("s t q -> s q t"), vs_col[:, 1:].unsqueeze(1).to_broadcast([P, NQ // 2, 3]), MULT)

        l_0 = held.tile([P, 1], F32, name="l_0")
        p_summed = held.tile([P, N + 1], F32, name="p_summed")
        nc.scalar.activation(p_summed[:], p_sb[:], COPY, accum_out=l_0[:])

        v_b = held.tile([P, DV * 4], BF16, name="v_b", align_bytes=64)
        for c in halves:
            nc.scalar.copy(v_b[:].bitcast(F32).rearrange("p (e u) -> p e u", u=2)[:, c, :], v_ps[:, :, c].rearrange("p u e -> p e u"))

        for c in halves:
            nc.vector.quantize_mx(out=w_c[:, c].bitcast(FP8X4), scales=w_s[:, c], in_=w_b[:, c, :].rearrange("p q t -> p (q t)"))
        v_c = held.tile([P, DV], U32, name="v_c", align_bytes=64)
        v_s = held.tile([P, DV], U8, name="v_s", align_bytes=64)
        for c in halves:
            nc.vector.quantize_mx(out=v_c[:, c].bitcast(FP8X4), scales=v_s[:, c], in_=v_b[:, 4 * c.start : 4 * c.stop])

        y_ps = psum.tile([P, DV], F32, name="y_ps")
        nc.tensor.matmul_mx(y_ps[:], lhsT=w_c[:].bitcast(FP8X4), lhsT_scale=w_s[:], rhs=v_c[:].bitcast(FP8X4), rhs_scale=v_s[:], start=True, stop=True)

        r_l = held.tile([P, 1], F32, name="r_l", tag="w_b", align_bytes=64)
        nc.vector.reciprocal(r_l[:], l_0[:])

        y_sb = held.tile([P, DV], F32, name="y_sb")
        nc.vector.tensor_scalar(y_sb[:], y_ps[:], r_l[:], None, op0=MULT)
        nc.sync.dma_start(out.rearrange("b q e -> (b q) e"), y_sb[:])
